import numpy as np
import ml_dtypes


def mxq(x, axis, fmt="e4m3"):
    dtype, down = {"e4m3": (ml_dtypes.float8_e4m3fn, 7), "e5m2": (ml_dtypes.float8_e5m2, 14)}[fmt]
    v = np.moveaxis(np.asarray(x, np.float32).astype(ml_dtypes.bfloat16).astype(np.float64), axis, -1)
    blocks = v.reshape(v.shape[:-1] + (-1, 32))
    amax = np.abs(blocks).max(-1, keepdims=True)
    byte = np.maximum(np.where(amax > 0, np.frexp(amax)[1] - 1 + 127, 0) - down, 1)
    scale = np.exp2(byte - 127.0)
    codes = (blocks / scale).astype(np.float32).astype(dtype).astype(np.float64)
    return np.moveaxis((codes * scale).reshape(v.shape), -1, axis)


WIDE = False


def mx_kscale(k):
    if not WIDE:
        return np.ones(k)
    levels = np.array([10, -10, 5, -5, 0])
    if k % 512:
        return np.exp2(np.random.permutation(np.resize(levels, k // 32))).repeat(32)
    a = np.empty((k // 512, 16))
    for p in range(k // 512):
        a[p, :8] = np.random.permutation(np.resize(levels, 8))
        for g in range(8):
            far = levels[np.abs(levels - a[p, g]) >= 10]
            a[p, g + 8] = far[np.random.randint(len(far))]
    return np.exp2(a.ravel()).repeat(32)


def f64(x):
    return np.asarray(x).astype(np.float64)


def striped(idx):
    return np.tile(idx.reshape(-1, 16).T, (8, 1)).astype(np.uint16)


def unstriped(offs):
    return offs[:16].T.reshape(-1).astype(np.int64)


def pack_weight(w):
    k, n = w.shape
    w = f64(np.asarray(w, np.float32).astype(ml_dtypes.bfloat16)).reshape(k // 32, 32, n)
    amax = np.abs(w).max(1)
    byte = np.clip(np.where(amax > 0, np.frexp(amax)[1] - 1 + 127 - 7, 1), 1, 254)
    scaled = (w * np.exp2(127.0 - byte)[:, None, :]).reshape(k, n).astype(np.float32)
    words = np.ascontiguousarray(scaled.reshape(k // 512, 128, 4, n).transpose(0, 1, 3, 2)).astype(ml_dtypes.float8_e4m3fn).view(np.uint8)
    return words, np.ascontiguousarray(byte.astype(np.uint8).reshape(k // 512, 16, n))


def unpack_weight(words, scales):
    g, p, n, _ = words.shape
    vals = np.ascontiguousarray(words).view(ml_dtypes.float8_e4m3fn).astype(np.float64) * np.repeat(np.exp2(scales.astype(np.float64) - 127.0), 8, axis=1)[..., None]
    return vals.transpose(0, 1, 3, 2).reshape(g * 512, n)


E2M1 = np.array([0.0, 0.5, 1.0, 1.5, 2.0, 3.0, 4.0, 6.0, -0.0, -0.5, -1.0, -1.5, -2.0, -3.0, -4.0, -6.0])


def pack_fp4(w):
    k, n = w.shape
    w = f64(np.asarray(w, np.float32).astype(ml_dtypes.bfloat16)).reshape(k // 32, 32, n)
    amax = np.abs(w).max(1)
    mant, ex = np.frexp(amax / 6.0)
    byte = np.clip(np.where(amax > 0, np.where(mant > 0.5, ex, ex - 1) + 127, 1), 1, 254)
    scaled = (w * np.exp2(127.0 - byte)[:, None, :]).reshape(k, n).astype(np.float32)
    c = np.ascontiguousarray(scaled.reshape(k // 512, 128, 4, n).transpose(0, 1, 3, 2)).astype(ml_dtypes.float4_e2m1fn).view(np.uint8) & 0xF
    words = (c[..., 0::2] | (c[..., 1::2] << 4)).reshape(k // 512, 128, 2 * n)
    return np.ascontiguousarray(words), np.ascontiguousarray(byte.astype(np.uint8).reshape(k // 512, 16, n))


def unpack_fp4(words, scales):
    g, _, n = scales.shape
    words = np.ascontiguousarray(words).reshape(g, 128, n, 2)
    nib = np.empty((g, 128, n, 4), np.uint8)
    nib[..., 0::2] = words & 0xF
    nib[..., 1::2] = words >> 4
    vals = E2M1[nib] * np.repeat(np.exp2(scales.astype(np.float64) - 127.0), 8, axis=1)[..., None]
    return vals.transpose(0, 1, 3, 2).reshape(g * 512, n)


def relu(v):
    return np.maximum(v, 0.0)


K, T, S, V, N = 512, 4096, 1024, 512, 128


def setup_inputs():
    n = np.random.standard_normal
    s = mx_kscale(K)[:, None]
    packed_xT = pack_weight(n((K, T)) * s)
    packed_w1 = pack_fp4(n((K, N)) / np.sqrt(K) / s)
    packed_w2 = pack_fp4(n((K, N)) / np.sqrt(K) / s)
    return {
        "x_words": packed_xT[0],
        "x_scales": packed_xT[1],
        "sT": (n((K, V)) * s).astype(np.float32),
        "w1_words": packed_w1[0],
        "w1_scales": packed_w1[1],
        "w2_words": packed_w2[0],
        "w2_scales": packed_w2[1],
        "offs": striped(np.random.permutation(T)[:S]),
        "par": striped(np.random.randint(0, V, S)),
    }


def reference(x_words, x_scales, sT, w1_words, w1_scales, w2_words, w2_scales, offs, par):
    xq = unpack_weight(x_words, x_scales)[:, unstriped(offs)]
    y = unpack_fp4(w1_words, w1_scales).T @ xq
    t = unpack_fp4(w2_words, w2_scales).T @ mxq(f64(sT), 0, "e4m3")
    return relu(y + t[:, unstriped(par)])

@@ -1,0 +1,139 @@
+from contextlib import ExitStack
+
+import concourse.mybir as mybir
+
+K, T, S, V, N = 512, 4096, 1024, 512, 128
+FLOPS = 2 * K * N * (S + V)
+
+F32 = mybir.dt.float32
+BF16 = mybir.dt.bfloat16
+I32 = mybir.dt.int32
+U32 = mybir.dt.uint32
+U16 = mybir.dt.uint16
+U8 = mybir.dt.uint8
+FP8X4 = mybir.dt.float8_e4m3fn_x4
+FP4X4 = mybir.dt.float4_e2m1fn_x4
+ADD = mybir.AluOpType.add
+RELU = mybir.ActivationFunctionType.Relu
+
+P = 128
+PACK = 4
+GROUP = 16
+HALF = S // 2
+V_HALF = V // 2
+T_PAD = 16
+
+
+def tile_picked_fpn_relu_p_kernel(
+    tc, x_words, x_scales, sT, w1_words, w1_scales, w2_words, w2_scales, offs, par, out
+):
+    nc = tc.nc
+    with ExitStack() as ctx:
+        keep = ctx.enter_context(tc.tile_pool(name="keep", bufs=1))
+        psum = ctx.enter_context(tc.psum_pool(name="psum", bufs=1))
+
+        offs_sb = keep.tile([P, S // GROUP], U16, name="offs_sb")
+        par_sb = keep.tile([P, S // GROUP], U16, name="par_sb")
+        xw_sb = keep.tile([P, T], U32, name="xw_sb", align_bytes=64)
+        xs_sb = keep.tile([P, T], U8, name="xs_sb", align_bytes=64)
+        s_raw = [keep.tile([P, PACK, V_HALF], F32, name=f"s_raw{h}", align_bytes=64) for h in range(2)]
+        w1w = keep.tile([P, 2 * N], U8, name="w1w", align_bytes=64)
+        w2w = keep.tile([P, 2 * N], U8, name="w2w", align_bytes=64)
+        w1s = keep.tile([P, N], U8, name="w1s", align_bytes=64)
+        w2s = keep.tile([P, N], U8, name="w2s", align_bytes=64)
+        xs_picked = keep.tile([P, S], U8, name="xs_picked", align_bytes=64)
+        xs_plane = keep.tile([P, S], U8, name="xs_plane", align_bytes=64)
+        t_sb = keep.tile([P, V + T_PAD], F32, name="t_sb", align_bytes=64)
+
+        nc.vector.memset(xs_sb[0:112, :].bitcast(I32), 0)
+        nc.vector.memset(t_sb[:, V:], 0.0)
+
+        s_rows = sT.rearrange("(p j) v -> p j v", j=PACK)
+        nc.sync.dma_start(offs_sb[:], offs)
+        nc.sync.dma_start(xs_sb[112:P, :].bitcast(I32), x_scales[0].bitcast(I32))
+        for q in range(4):
+            nc.scalar.dma_start(
+                w2s[32 * q : 32 * q + 4, :].bitcast(I32), w2_scales[0, 4 * q : 4 * q + 4, :].bitcast(I32)
+            )
+        for h in range(2):
+            nc.sync.dma_start(s_raw[h][:], s_rows[:, :, h * V_HALF : (h + 1) * V_HALF])
+        nc.sync.dma_start(par_sb[:], par)
+        for q in range(2):
+            nc.sync.dma_start(
+                w1s[32 * q : 32 * q + 4, :].bitcast(I32), w1_scales[0, 4 * q : 4 * q + 4, :].bitcast(I32)
+            )
+        nc.sync.dma_start(xw_sb[:].bitcast(I32), x_words[0].rearrange("p n r -> p (n r)").bitcast(I32))
+        for q in range(2, 4):
+            nc.sync.dma_start(
+                w1s[32 * q : 32 * q + 4, :].bitcast(I32), w1_scales[0, 4 * q : 4 * q + 4, :].bitcast(I32)
+            )
+        nc.gpsimd.dma_start(w2w[:].bitcast(I32), w2_words[0].bitcast(I32))
+        nc.gpsimd.dma_start(w1w[:].bitcast(I32), w1_words[0].bitcast(I32))
+
+        nc.vector.tensor_copy(xs_picked[:], xs_sb[:].indirect(offs_sb[:]))
+        for q in range(4):
+            nc.sync.dma_start(
+                xs_plane[32 * q : 32 * q + 4, :].bitcast(I32),
+                xs_picked[112 + 4 * q : 116 + 4 * q, :].bitcast(I32),
+            )
+
+        grouped = [keep.tile([P, V_HALF, PACK], BF16, name=f"grouped{h}", align_bytes=64) for h in range(2)]
+        s_codes = [keep.tile([P, V_HALF], U32, name=f"s_codes{h}", align_bytes=64) for h in range(2)]
+        s_scales = [keep.tile([P, V_HALF], U8, name=f"s_scales{h}", align_bytes=64) for h in range(2)]
+        for h, c0, c1, on_scalar in [(0, 0, 256, True), (1, 0, 128, True), (1, 128, 256, False)]:
+            dst = grouped[h][:, c0:c1, :].rearrange("p (c i) j -> p c j i", i=4)
+            src = s_raw[h][:, :, c0:c1].rearrange("p j (c i) -> p c j i", i=4)
+            if on_scalar:
+                nc.scalar.copy(dst, src)
+            else:
+                nc.vector.tensor_copy(dst, src)
+        for h in range(2):
+            nc.vector.quantize_mx(
+                out=s_codes[h][:].bitcast(FP8X4),
+                scales=s_scales[h][:],
+                in_=grouped[h][:].rearrange("p c j -> p (c j)"),
+            )
+        for h in range(2):
+            t_ps = psum.tile([P, V_HALF], F32, name=f"t_ps{h}")
+            nc.tensor.matmul_mx(
+                out=t_ps[:],
+                lhsT=w2w[:].bitcast(FP4X4),
+                lhsT_scale=w2s[:],
+                rhs=s_codes[h][:].bitcast(FP8X4),
+                rhs_scale=s_scales[h][:],
+                start=True,
+                stop=True,
+            )
+            nc.scalar.copy(t_sb[:, h * V_HALF : (h + 1) * V_HALF], t_ps[:])
+
+        lists = [slice(h * HALF // GROUP, (h + 1) * HALF // GROUP) for h in range(2)]
+        t_picked = [keep.tile([P, HALF], F32, name=f"t_picked{h}", align_bytes=64) for h in range(2)]
+        xw_picked = [keep.tile([P, HALF], U32, name=f"xw_picked{h}", align_bytes=64) for h in range(2)]
+        for h in range(2):
+            nc.vector.tensor_copy(t_picked[h][:], t_sb[:].indirect(par_sb[:, lists[h]]))
+        for h in range(2):
+            nc.vector.tensor_copy(xw_picked[h][:], xw_sb[:].indirect(offs_sb[:, lists[h]]))
+
+        pieces = [(0, 0, 512), (1, 0, 256), (1, 256, 256)]
+        sums = []
+        for i, (h, c0, width) in enumerate(pieces):
+            y_ps = psum.tile([P, width], F32, name=f"y_ps{i}")
+            nc.tensor.matmul_mx(
+                out=y_ps[:],
+                lhsT=w1w[:].bitcast(FP4X4),
+                lhsT_scale=w1s[:],
+                rhs=xw_picked[h][:, c0 : c0 + width].bitcast(FP8X4),
+                rhs_scale=xs_plane[:, h * HALF + c0 : h * HALF + c0 + width],
+                start=True,
+                stop=True,
+            )
+            total = keep.tile([P, width], F32, name=f"total{i}", align_bytes=64)
+            nc.vector.tensor_tensor(total[:], y_ps[:], t_picked[h][:, c0 : c0 + width], ADD)
+            sums.append(total)
+        for i, (h, c0, width) in enumerate(pieces):
+            result = keep.tile([P, width], F32, name=f"result{i}", align_bytes=64)
+            if h == 0:
+                nc.scalar.activation(result[:], sums[i][:], RELU)
+            else:
+                nc.vector.tensor_scalar_max(result[:], sums[i][:], 0.0)
+            nc.sync.dma_start(out[:, h * HALF + c0 : h * HALF + c0 + width], result[:])

@@ -36,7 +36,7 @@ def tile_picked_fpn_relu_p_kernel(
         par_sb = keep.tile([P, S // GROUP], U16, name="par_sb")
         xw_sb = keep.tile([P, T], U32, name="xw_sb", align_bytes=64)
         xs_sb = keep.tile([P, T], U8, name="xs_sb", align_bytes=64)
-        s_raw = [keep.tile([P, PACK, V_HALF], F32, name=f"s_raw{h}", align_bytes=64) for h in range(2)]
+        s_raw = keep.tile([P, PACK, V], F32, name="s_raw", align_bytes=64)
         w1w = keep.tile([P, 2 * N], U8, name="w1w", align_bytes=64)
         w2w = keep.tile([P, 2 * N], U8, name="w2w", align_bytes=64)
         w1s = keep.tile([P, N], U8, name="w1s", align_bytes=64)
@@ -55,20 +55,16 @@ def tile_picked_fpn_relu_p_kernel(
             nc.scalar.dma_start(
                 w2s[32 * q : 32 * q + 4, :].bitcast(I32), w2_scales[0, 4 * q : 4 * q + 4, :].bitcast(I32)
             )
-        for h in range(2):
-            nc.sync.dma_start(s_raw[h][:], s_rows[:, :, h * V_HALF : (h + 1) * V_HALF])
+        nc.sync.dma_start(s_raw[:], s_rows)
         nc.sync.dma_start(par_sb[:], par)
-        for q in range(2):
-            nc.sync.dma_start(
-                w1s[32 * q : 32 * q + 4, :].bitcast(I32), w1_scales[0, 4 * q : 4 * q + 4, :].bitcast(I32)
-            )
         nc.sync.dma_start(xw_sb[:].bitcast(I32), x_words[0].rearrange("p n r -> p (n r)").bitcast(I32))
-        for q in range(2, 4):
+        for q in range(1, 4):
             nc.sync.dma_start(
                 w1s[32 * q : 32 * q + 4, :].bitcast(I32), w1_scales[0, 4 * q : 4 * q + 4, :].bitcast(I32)
             )
         nc.gpsimd.dma_start(w2w[:].bitcast(I32), w2_words[0].bitcast(I32))
         nc.gpsimd.dma_start(w1w[:].bitcast(I32), w1_words[0].bitcast(I32))
+        nc.gpsimd.dma_start(w1s[0:4, :].bitcast(I32), w1_scales[0, 0:4, :].bitcast(I32))
 
         nc.vector.tensor_copy(xs_picked[:], xs_sb[:].indirect(offs_sb[:]))
         for q in range(4):
@@ -77,34 +73,35 @@ def tile_picked_fpn_relu_p_kernel(
                 xs_picked[112 + 4 * q : 116 + 4 * q, :].bitcast(I32),
             )
 
-        grouped = [keep.tile([P, V_HALF, PACK], BF16, name=f"grouped{h}", align_bytes=64) for h in range(2)]
-        s_codes = [keep.tile([P, V_HALF], U32, name=f"s_codes{h}", align_bytes=64) for h in range(2)]
-        s_scales = [keep.tile([P, V_HALF], U8, name=f"s_scales{h}", align_bytes=64) for h in range(2)]
-        for h, c0, c1, on_scalar in [(0, 0, 256, True), (1, 0, 128, True), (1, 128, 256, False)]:
-            dst = grouped[h][:, c0:c1, :].rearrange("p (c i) j -> p c j i", i=4)
-            src = s_raw[h][:, :, c0:c1].rearrange("p j (c i) -> p c j i", i=4)
+        grouped = keep.tile([P, V * PACK], BF16, name="grouped", align_bytes=64)
+        s_codes = keep.tile([P, V], U32, name="s_codes", align_bytes=64)
+        s_scales = keep.tile([P, V], U8, name="s_scales", align_bytes=64)
+        for c0, c1, on_scalar in [(0, 256, False), (256, 416, True), (416, 512, False)]:
+            dst = grouped[:, PACK * c0 : PACK * c1].rearrange("p (c i j) -> p c j i", i=4, j=PACK)
+            src = s_raw[:, :, c0:c1].rearrange("p j (c i) -> p c j i", i=4)
             if on_scalar:
                 nc.scalar.copy(dst, src)
             else:
                 nc.vector.tensor_copy(dst, src)
-        for h in range(2):
+        cells = [(0, 256), (256, 384), (384, 512)]
+        for c0, c1 in cells:
             nc.vector.quantize_mx(
-                out=s_codes[h][:].bitcast(FP8X4),
-                scales=s_scales[h][:],
-                in_=grouped[h][:].rearrange("p c j -> p (c j)"),
+                out=s_codes[:, c0:c1].bitcast(FP8X4),
+                scales=s_scales[:, c0:c1],
+                in_=grouped[:, PACK * c0 : PACK * c1],
             )
-        for h in range(2):
-            t_ps = psum.tile([P, V_HALF], F32, name=f"t_ps{h}")
+        for c0, c1 in cells:
+            t_ps = psum.tile([P, c1 - c0], F32, name=f"t_ps{c0}")
             nc.tensor.matmul_mx(
                 out=t_ps[:],
                 lhsT=w2w[:].bitcast(FP4X4),
                 lhsT_scale=w2s[:],
-                rhs=s_codes[h][:].bitcast(FP8X4),
-                rhs_scale=s_scales[h][:],
+                rhs=s_codes[:, c0:c1].bitcast(FP8X4),
+                rhs_scale=s_scales[:, c0:c1],
                 start=True,
                 stop=True,
             )
-            nc.scalar.copy(t_sb[:, h * V_HALF : (h + 1) * V_HALF], t_ps[:])
+            nc.scalar.copy(t_sb[:, c0:c1], t_ps[:])
 
         lists = [slice(h * HALF // GROUP, (h + 1) * HALF // GROUP) for h in range(2)]
         t_picked = [keep.tile([P, HALF], F32, name=f"t_picked{h}", align_bytes=64) for h in range(2)]

@@ -22,6 +22,7 @@ GROUP = 16
 HALF = S // 2
 V_HALF = V // 2
 T_PAD = 16
+SPLIT = 96
 
 
 def tile_picked_fpn_relu_p_kernel(
@@ -36,13 +37,12 @@ def tile_picked_fpn_relu_p_kernel(
         par_sb = keep.tile([P, S // GROUP], U16, name="par_sb")
         xw_sb = keep.tile([P, T], U32, name="xw_sb", align_bytes=64)
         xs_sb = keep.tile([P, T], U8, name="xs_sb", align_bytes=64)
-        s_raw = keep.tile([P, PACK, V], F32, name="s_raw", align_bytes=64)
+        s_raw = [keep.tile([P, PACK, V_HALF], F32, name=f"s_raw{h}", align_bytes=64) for h in range(2)]
         w1w = keep.tile([P, 2 * N], U8, name="w1w", align_bytes=64)
         w2w = keep.tile([P, 2 * N], U8, name="w2w", align_bytes=64)
         w1s = keep.tile([P, N], U8, name="w1s", align_bytes=64)
         w2s = keep.tile([P, N], U8, name="w2s", align_bytes=64)
-        xs_picked = keep.tile([P, S], U8, name="xs_picked", align_bytes=64)
-        xs_plane = keep.tile([P, S], U8, name="xs_plane", align_bytes=64)
+        xs_plane = [keep.tile([P, HALF], U8, name=f"xs_plane{h}", align_bytes=64) for h in range(2)]
         t_sb = keep.tile([P, V + T_PAD], F32, name="t_sb", align_bytes=64)
 
         nc.vector.memset(xs_sb[0:112, :].bitcast(I32), 0)
@@ -55,55 +55,67 @@ def tile_picked_fpn_relu_p_kernel(
             nc.scalar.dma_start(
                 w2s[32 * q : 32 * q + 4, :].bitcast(I32), w2_scales[0, 4 * q : 4 * q + 4, :].bitcast(I32)
             )
-        nc.sync.dma_start(s_raw[:], s_rows)
+        for h in range(2):
+            nc.sync.dma_start(s_raw[h][:], s_rows[:, :, h * V_HALF : (h + 1) * V_HALF])
         nc.sync.dma_start(par_sb[:], par)
+        for q in range(2):
+            nc.sync.dma_start(
+                w1s[32 * q : 32 * q + 4, :].bitcast(I32), w1_scales[0, 4 * q : 4 * q + 4, :].bitcast(I32)
+            )
         nc.sync.dma_start(xw_sb[:].bitcast(I32), x_words[0].rearrange("p n r -> p (n r)").bitcast(I32))
-        for q in range(1, 4):
+        for q in range(2, 4):
             nc.sync.dma_start(
                 w1s[32 * q : 32 * q + 4, :].bitcast(I32), w1_scales[0, 4 * q : 4 * q + 4, :].bitcast(I32)
             )
         nc.gpsimd.dma_start(w2w[:].bitcast(I32), w2_words[0].bitcast(I32))
         nc.gpsimd.dma_start(w1w[:].bitcast(I32), w1_words[0].bitcast(I32))
-        nc.gpsimd.dma_start(w1s[0:4, :].bitcast(I32), w1_scales[0, 0:4, :].bitcast(I32))
 
-        nc.vector.tensor_copy(xs_picked[:], xs_sb[:].indirect(offs_sb[:]))
-        for q in range(4):
-            nc.sync.dma_start(
-                xs_plane[32 * q : 32 * q + 4, :].bitcast(I32),
-                xs_picked[112 + 4 * q : 116 + 4 * q, :].bitcast(I32),
-            )
+        lists = [slice(h * HALF // GROUP, (h + 1) * HALF // GROUP) for h in range(2)]
 
-        grouped = keep.tile([P, V * PACK], BF16, name="grouped", align_bytes=64)
-        s_codes = keep.tile([P, V], U32, name="s_codes", align_bytes=64)
-        s_scales = keep.tile([P, V], U8, name="s_scales", align_bytes=64)
-        for c0, c1, on_scalar in [(0, 256, False), (256, 416, True), (416, 512, False)]:
-            dst = grouped[:, PACK * c0 : PACK * c1].rearrange("p (c i j) -> p c j i", i=4, j=PACK)
-            src = s_raw[:, :, c0:c1].rearrange("p j (c i) -> p c j i", i=4)
-            if on_scalar:
-                nc.scalar.copy(dst, src)
-            else:
-                nc.vector.tensor_copy(dst, src)
-        cells = [(0, 256), (256, 384), (384, 512)]
-        for c0, c1 in cells:
+        def pick_scales(h, tag):
+            picked = keep.tile([P, HALF], U8, name=f"xs_picked{h}", tag=tag, align_bytes=64)
+            nc.vector.tensor_copy(picked[:], xs_sb[:].indirect(offs_sb[:, lists[h]]))
+            for q in range(4):
+                nc.sync.dma_start(
+                    xs_plane[h][32 * q : 32 * q + 4, :].bitcast(I32),
+                    picked[112 + 4 * q : 116 + 4 * q, :].bitcast(I32),
+                )
+
+        pick_scales(0, "first")
+
+        grouped = [
+            keep.tile([P, V_HALF, PACK], BF16, name=f"grouped{h}", tag=f"grouped{h}", align_bytes=64) for h in range(2)
+        ]
+        s_codes = [keep.tile([P, V_HALF], U32, name=f"s_codes{h}", align_bytes=64) for h in range(2)]
+        s_scales = [keep.tile([P, V_HALF], U8, name=f"s_scales{h}", align_bytes=64) for h in range(2)]
+        for h in range(2):
+            for c0, c1, on_scalar in [(0, SPLIT, True), (SPLIT, V_HALF, False)]:
+                dst = grouped[h][:, c0:c1, :].rearrange("p (c i) j -> p c j i", i=4)
+                src = s_raw[h][:, :, c0:c1].rearrange("p j (c i) -> p c j i", i=4)
+                if on_scalar:
+                    nc.scalar.copy(dst, src)
+                else:
+                    nc.vector.tensor_copy(dst, src)
             nc.vector.quantize_mx(
-                out=s_codes[:, c0:c1].bitcast(FP8X4),
-                scales=s_scales[:, c0:c1],
-                in_=grouped[:, PACK * c0 : PACK * c1],
+                out=s_codes[h][:].bitcast(FP8X4),
+                scales=s_scales[h][:],
+                in_=grouped[h][:].rearrange("p c j -> p (c j)"),
             )
-        for c0, c1 in cells:
-            t_ps = psum.tile([P, c1 - c0], F32, name=f"t_ps{c0}")
+        for h in range(2):
+            t_ps = psum.tile([P, V_HALF], F32, name=f"t_ps{h}")
             nc.tensor.matmul_mx(
                 out=t_ps[:],
                 lhsT=w2w[:].bitcast(FP4X4),
                 lhsT_scale=w2s[:],
-                rhs=s_codes[:, c0:c1].bitcast(FP8X4),
-                rhs_scale=s_scales[:, c0:c1],
+                rhs=s_codes[h][:].bitcast(FP8X4),
+                rhs_scale=s_scales[h][:],
                 start=True,
                 stop=True,
             )
-            nc.scalar.copy(t_sb[:, c0:c1], t_ps[:])
+            nc.scalar.copy(t_sb[:, h * V_HALF : (h + 1) * V_HALF], t_ps[:])
 
-        lists = [slice(h * HALF // GROUP, (h + 1) * HALF // GROUP) for h in range(2)]
+        pick_scales(1, "grouped1")
+
         t_picked = [keep.tile([P, HALF], F32, name=f"t_picked{h}", align_bytes=64) for h in range(2)]
         xw_picked = [keep.tile([P, HALF], U32, name=f"xw_picked{h}", align_bytes=64) for h in range(2)]
         for h in range(2):
@@ -111,7 +123,7 @@ def tile_picked_fpn_relu_p_kernel(
         for h in range(2):
             nc.vector.tensor_copy(xw_picked[h][:], xw_sb[:].indirect(offs_sb[:, lists[h]]))
 
-        pieces = [(0, 0, 512), (1, 0, 256), (1, 256, 256)]
+        pieces = [(0, 0, 256), (0, 256, 256), (1, 0, 256), (1, 256, 256)]
         sums = []
         for i, (h, c0, width) in enumerate(pieces):
             y_ps = psum.tile([P, width], F32, name=f"y_ps{i}")
@@ -120,7 +132,7 @@ def tile_picked_fpn_relu_p_kernel(
                 lhsT=w1w[:].bitcast(FP4X4),
                 lhsT_scale=w1s[:],
                 rhs=xw_picked[h][:, c0 : c0 + width].bitcast(FP8X4),
-                rhs_scale=xs_plane[:, h * HALF + c0 : h * HALF + c0 + width],
+                rhs_scale=xs_plane[h][:, c0 : c0 + width],
                 start=True,
                 stop=True,
             )
@@ -129,7 +141,7 @@ def tile_picked_fpn_relu_p_kernel(
             sums.append(total)
         for i, (h, c0, width) in enumerate(pieces):
             result = keep.tile([P, width], F32, name=f"result{i}", align_bytes=64)
-            if h == 0:
+            if i < 3:
                 nc.scalar.activation(result[:], sums[i][:], RELU)
             else:
                 nc.vector.tensor_scalar_max(result[:], sums[i][:], 0.0)

@@ -22,7 +22,6 @@ GROUP = 16
 HALF = S // 2
 V_HALF = V // 2
 T_PAD = 16
-SPLIT = 96
 
 
 def tile_picked_fpn_relu_p_kernel(
@@ -42,7 +41,8 @@ def tile_picked_fpn_relu_p_kernel(
         w2w = keep.tile([P, 2 * N], U8, name="w2w", align_bytes=64)
         w1s = keep.tile([P, N], U8, name="w1s", align_bytes=64)
         w2s = keep.tile([P, N], U8, name="w2s", align_bytes=64)
-        xs_plane = [keep.tile([P, HALF], U8, name=f"xs_plane{h}", align_bytes=64) for h in range(2)]
+        xs_picked = keep.tile([P, S], U8, name="xs_picked", align_bytes=64)
+        xs_plane = keep.tile([P, S], U8, name="xs_plane", align_bytes=64)
         t_sb = keep.tile([P, V + T_PAD], F32, name="t_sb", align_bytes=64)
 
         nc.vector.memset(xs_sb[0:112, :].bitcast(I32), 0)
@@ -58,44 +58,33 @@ def tile_picked_fpn_relu_p_kernel(
         for h in range(2):
             nc.sync.dma_start(s_raw[h][:], s_rows[:, :, h * V_HALF : (h + 1) * V_HALF])
         nc.sync.dma_start(par_sb[:], par)
-        for q in range(2):
-            nc.sync.dma_start(
-                w1s[32 * q : 32 * q + 4, :].bitcast(I32), w1_scales[0, 4 * q : 4 * q + 4, :].bitcast(I32)
-            )
         nc.sync.dma_start(xw_sb[:].bitcast(I32), x_words[0].rearrange("p n r -> p (n r)").bitcast(I32))
-        for q in range(2, 4):
+        for q in range(1, 4):
             nc.sync.dma_start(
                 w1s[32 * q : 32 * q + 4, :].bitcast(I32), w1_scales[0, 4 * q : 4 * q + 4, :].bitcast(I32)
             )
         nc.gpsimd.dma_start(w2w[:].bitcast(I32), w2_words[0].bitcast(I32))
         nc.gpsimd.dma_start(w1w[:].bitcast(I32), w1_words[0].bitcast(I32))
+        nc.gpsimd.dma_start(w1s[0:4, :].bitcast(I32), w1_scales[0, 0:4, :].bitcast(I32))
 
-        lists = [slice(h * HALF // GROUP, (h + 1) * HALF // GROUP) for h in range(2)]
+        nc.vector.tensor_copy(xs_picked[:], xs_sb[:].indirect(offs_sb[:]))
+        for q in range(4):
+            nc.sync.dma_start(
+                xs_plane[32 * q : 32 * q + 4, :].bitcast(I32),
+                xs_picked[112 + 4 * q : 116 + 4 * q, :].bitcast(I32),
+            )
 
-        def pick_scales(h, tag):
-            picked = keep.tile([P, HALF], U8, name=f"xs_picked{h}", tag=tag, align_bytes=64)
-            nc.vector.tensor_copy(picked[:], xs_sb[:].indirect(offs_sb[:, lists[h]]))
-            for q in range(4):
-                nc.sync.dma_start(
-                    xs_plane[h][32 * q : 32 * q + 4, :].bitcast(I32),
-                    picked[112 + 4 * q : 116 + 4 * q, :].bitcast(I32),
-                )
-
-        pick_scales(0, "first")
-
-        grouped = [
-            keep.tile([P, V_HALF, PACK], BF16, name=f"grouped{h}", tag=f"grouped{h}", align_bytes=64) for h in range(2)
-        ]
+        grouped = [keep.tile([P, V_HALF, PACK], BF16, name=f"grouped{h}", align_bytes=64) for h in range(2)]
         s_codes = [keep.tile([P, V_HALF], U32, name=f"s_codes{h}", align_bytes=64) for h in range(2)]
         s_scales = [keep.tile([P, V_HALF], U8, name=f"s_scales{h}", align_bytes=64) for h in range(2)]
+        for h, c0, c1, on_scalar in [(0, 0, 256, True), (1, 0, 128, True), (1, 128, 256, False)]:
+            dst = grouped[h][:, c0:c1, :].rearrange("p (c i) j -> p c j i", i=4)
+            src = s_raw[h][:, :, c0:c1].rearrange("p j (c i) -> p c j i", i=4)
+            if on_scalar:
+                nc.scalar.copy(dst, src)
+            else:
+                nc.vector.tensor_copy(dst, src)
         for h in range(2):
-            for c0, c1, on_scalar in [(0, SPLIT, True), (SPLIT, V_HALF, False)]:
-                dst = grouped[h][:, c0:c1, :].rearrange("p (c i) j -> p c j i", i=4)
-                src = s_raw[h][:, :, c0:c1].rearrange("p j (c i) -> p c j i", i=4)
-                if on_scalar:
-                    nc.scalar.copy(dst, src)
-                else:
-                    nc.vector.tensor_copy(dst, src)
             nc.vector.quantize_mx(
                 out=s_codes[h][:].bitcast(FP8X4),
                 scales=s_scales[h][:],
@@ -114,8 +103,7 @@ def tile_picked_fpn_relu_p_kernel(
             )
             nc.scalar.copy(t_sb[:, h * V_HALF : (h + 1) * V_HALF], t_ps[:])
 
-        pick_scales(1, "grouped1")
-
+        lists = [slice(h * HALF // GROUP, (h + 1) * HALF // GROUP) for h in range(2)]
         t_picked = [keep.tile([P, HALF], F32, name=f"t_picked{h}", align_bytes=64) for h in range(2)]
         xw_picked = [keep.tile([P, HALF], U32, name=f"xw_picked{h}", align_bytes=64) for h in range(2)]
         for h in range(2):
@@ -132,7 +120,7 @@ def tile_picked_fpn_relu_p_kernel(
                 lhsT=w1w[:].bitcast(FP4X4),
                 lhsT_scale=w1s[:],
                 rhs=xw_picked[h][:, c0 : c0 + width].bitcast(FP8X4),
-                rhs_scale=xs_plane[h][:, c0 : c0 + width],
+                rhs_scale=xs_plane[:, h * HALF + c0 : h * HALF + c0 + width],
                 start=True,
                 stop=True,
             )

@@ -36,36 +36,33 @@ def tile_picked_fpn_relu_p_kernel(
         par_sb = keep.tile([P, S // GROUP], U16, name="par_sb")
         xw_sb = keep.tile([P, T], U32, name="xw_sb", align_bytes=64)
         xs_sb = keep.tile([P, T], U8, name="xs_sb", align_bytes=64)
-        s_raw = [keep.tile([P, PACK, V_HALF], F32, name=f"s_raw{h}", align_bytes=64) for h in range(2)]
+        s_raw = [keep.tile([P, PACK, V_HALF], F32, name=f"s_raw{h}", tag=f"s_raw{h}", align_bytes=64) for h in range(2)]
         w1w = keep.tile([P, 2 * N], U8, name="w1w", align_bytes=64)
         w2w = keep.tile([P, 2 * N], U8, name="w2w", align_bytes=64)
         w1s = keep.tile([P, N], U8, name="w1s", align_bytes=64)
         w2s = keep.tile([P, N], U8, name="w2s", align_bytes=64)
         xs_picked = keep.tile([P, S], U8, name="xs_picked", align_bytes=64)
         xs_plane = keep.tile([P, S], U8, name="xs_plane", align_bytes=64)
-        t_sb = keep.tile([P, V + T_PAD], F32, name="t_sb", align_bytes=64)
 
         nc.vector.memset(xs_sb[0:112, :].bitcast(I32), 0)
-        nc.vector.memset(t_sb[:, V:], 0.0)
 
         s_rows = sT.rearrange("(p j) v -> p j v", j=PACK)
+        def load_scale_rows(queue, plane, scales, q):
+            queue.dma_start(plane[32 * q : 32 * q + 4, :].bitcast(I32), scales[0, 4 * q : 4 * q + 4, :].bitcast(I32))
+
         nc.sync.dma_start(offs_sb[:], offs)
         nc.sync.dma_start(xs_sb[112:P, :].bitcast(I32), x_scales[0].bitcast(I32))
-        for q in range(4):
-            nc.scalar.dma_start(
-                w2s[32 * q : 32 * q + 4, :].bitcast(I32), w2_scales[0, 4 * q : 4 * q + 4, :].bitcast(I32)
-            )
         for h in range(2):
             nc.sync.dma_start(s_raw[h][:], s_rows[:, :, h * V_HALF : (h + 1) * V_HALF])
+        for q in range(4):
+            load_scale_rows(nc.sync, w2s, w2_scales, q)
         nc.sync.dma_start(par_sb[:], par)
         nc.sync.dma_start(xw_sb[:].bitcast(I32), x_words[0].rearrange("p n r -> p (n r)").bitcast(I32))
         for q in range(1, 4):
-            nc.sync.dma_start(
-                w1s[32 * q : 32 * q + 4, :].bitcast(I32), w1_scales[0, 4 * q : 4 * q + 4, :].bitcast(I32)
-            )
+            load_scale_rows(nc.sync, w1s, w1_scales, q)
         nc.gpsimd.dma_start(w2w[:].bitcast(I32), w2_words[0].bitcast(I32))
         nc.gpsimd.dma_start(w1w[:].bitcast(I32), w1_words[0].bitcast(I32))
-        nc.gpsimd.dma_start(w1s[0:4, :].bitcast(I32), w1_scales[0, 0:4, :].bitcast(I32))
+        load_scale_rows(nc.gpsimd, w1s, w1_scales, 0)
 
         nc.vector.tensor_copy(xs_picked[:], xs_sb[:].indirect(offs_sb[:]))
         for q in range(4):
@@ -90,6 +87,8 @@ def tile_picked_fpn_relu_p_kernel(
                 scales=s_scales[h][:],
                 in_=grouped[h][:].rearrange("p c j -> p (c j)"),
             )
+        t_sb = keep.tile([P, V + T_PAD], F32, name="t_sb", tag="s_raw1", align_bytes=64)
+        nc.vector.memset(t_sb[:, V:], 0.0)
         for h in range(2):
             t_ps = psum.tile([P, V_HALF], F32, name=f"t_ps{h}")
             nc.tensor.matmul_mx(

@@ -41,37 +41,44 @@ def tile_picked_fpn_relu_p_kernel(
         w2w = keep.tile([P, 2 * N], U8, name="w2w", align_bytes=64)
         w1s = keep.tile([P, N], U8, name="w1s", align_bytes=64)
         w2s = keep.tile([P, N], U8, name="w2s", align_bytes=64)
-        xs_picked = keep.tile([P, S], U8, name="xs_picked", align_bytes=64)
-        xs_plane = keep.tile([P, S], U8, name="xs_plane", align_bytes=64)
+        xs_plane = [keep.tile([P, HALF], U8, name=f"xs_plane{h}", align_bytes=64) for h in range(2)]
+        lists = [slice(h * HALF // GROUP, (h + 1) * HALF // GROUP) for h in range(2)]
 
-        nc.vector.memset(xs_sb[0:112, :].bitcast(I32), 0)
+        nc.vector.memset(xs_sb[:].bitcast(I32), 0)
 
         s_rows = sT.rearrange("(p j) v -> p j v", j=PACK)
         def load_scale_rows(queue, plane, scales, q):
             queue.dma_start(plane[32 * q : 32 * q + 4, :].bitcast(I32), scales[0, 4 * q : 4 * q + 4, :].bitcast(I32))
 
         nc.sync.dma_start(offs_sb[:], offs)
-        nc.sync.dma_start(xs_sb[112:P, :].bitcast(I32), x_scales[0].bitcast(I32))
-        for h in range(2):
-            nc.sync.dma_start(s_raw[h][:], s_rows[:, :, h * V_HALF : (h + 1) * V_HALF])
+        nc.sync.dma_start(par_sb[:], par)
+        nc.sync.dma_start(s_raw[0][:], s_rows[:, :, 0:V_HALF])
+        nc.sync.dma_start(xs_sb[32:96:4, :].bitcast(I32), x_scales[0].bitcast(I32))
+        nc.sync.dma_start(s_raw[1][:], s_rows[:, :, V_HALF:V])
         for q in range(4):
             load_scale_rows(nc.sync, w2s, w2_scales, q)
-        nc.sync.dma_start(par_sb[:], par)
         nc.sync.dma_start(xw_sb[:].bitcast(I32), x_words[0].rearrange("p n r -> p (n r)").bitcast(I32))
-        for q in range(1, 4):
+        for q in range(2, 4):
             load_scale_rows(nc.sync, w1s, w1_scales, q)
         nc.gpsimd.dma_start(w2w[:].bitcast(I32), w2_words[0].bitcast(I32))
         nc.gpsimd.dma_start(w1w[:].bitcast(I32), w1_words[0].bitcast(I32))
-        load_scale_rows(nc.gpsimd, w1s, w1_scales, 0)
+        for q in range(2):
+            load_scale_rows(nc.gpsimd, w1s, w1_scales, q)
 
-        nc.vector.tensor_copy(xs_picked[:], xs_sb[:].indirect(offs_sb[:]))
-        for q in range(4):
-            nc.sync.dma_start(
-                xs_plane[32 * q : 32 * q + 4, :].bitcast(I32),
-                xs_picked[112 + 4 * q : 116 + 4 * q, :].bitcast(I32),
-            )
+        def pick_scales(h, tag):
+            picked = keep.tile([P, HALF], U8, name=f"xs_picked{h}", tag=tag, align_bytes=64)
+            nc.vector.tensor_copy(picked[:], xs_sb[:].indirect(offs_sb[:, lists[h]]))
+            for q in range(4):
+                nc.sync.dma_start(
+                    xs_plane[h][32 * q : 32 * q + 4, :].bitcast(I32),
+                    picked[32 + 16 * q : 48 + 16 * q : 4, :].bitcast(I32),
+                )
 
-        grouped = [keep.tile([P, V_HALF, PACK], BF16, name=f"grouped{h}", align_bytes=64) for h in range(2)]
+        pick_scales(0, "xs_picked0")
+
+        grouped = [
+            keep.tile([P, V_HALF, PACK], BF16, name=f"grouped{h}", tag=f"grouped{h}", align_bytes=64) for h in range(2)
+        ]
         s_codes = [keep.tile([P, V_HALF], U32, name=f"s_codes{h}", align_bytes=64) for h in range(2)]
         s_scales = [keep.tile([P, V_HALF], U8, name=f"s_scales{h}", align_bytes=64) for h in range(2)]
         for h, c0, c1, on_scalar in [(0, 0, 256, True), (1, 0, 128, True), (1, 128, 256, False)]:
@@ -87,6 +94,7 @@ def tile_picked_fpn_relu_p_kernel(
                 scales=s_scales[h][:],
                 in_=grouped[h][:].rearrange("p c j -> p (c j)"),
             )
+        pick_scales(1, "grouped1")
         t_sb = keep.tile([P, V + T_PAD], F32, name="t_sb", tag="s_raw1", align_bytes=64)
         nc.vector.memset(t_sb[:, V:], 0.0)
         for h in range(2):
@@ -102,7 +110,6 @@ def tile_picked_fpn_relu_p_kernel(
             )
             nc.scalar.copy(t_sb[:, h * V_HALF : (h + 1) * V_HALF], t_ps[:])
 
-        lists = [slice(h * HALF // GROUP, (h + 1) * HALF // GROUP) for h in range(2)]
         t_picked = [keep.tile([P, HALF], F32, name=f"t_picked{h}", align_bytes=64) for h in range(2)]
         xw_picked = [keep.tile([P, HALF], U32, name=f"xw_picked{h}", align_bytes=64) for h in range(2)]
         for h in range(2):
@@ -119,7 +126,7 @@ def tile_picked_fpn_relu_p_kernel(
                 lhsT=w1w[:].bitcast(FP4X4),
                 lhsT_scale=w1s[:],
                 rhs=xw_picked[h][:, c0 : c0 + width].bitcast(FP8X4),
-                rhs_scale=xs_plane[:, h * HALF + c0 : h * HALF + c0 + width],
+                rhs_scale=xs_plane[h][:, c0 : c0 + width],
                 start=True,
                 stop=True,
             )

@@ -44,19 +44,19 @@ def tile_picked_fpn_relu_p_kernel(
         xs_plane = [keep.tile([P, HALF], U8, name=f"xs_plane{h}", align_bytes=64) for h in range(2)]
         lists = [slice(h * HALF // GROUP, (h + 1) * HALF // GROUP) for h in range(2)]
 
-        nc.vector.memset(xs_sb[:].bitcast(I32), 0)
+        nc.vector.memset(xs_sb[0:112, :].bitcast(I32), 0)
 
         s_rows = sT.rearrange("(p j) v -> p j v", j=PACK)
         def load_scale_rows(queue, plane, scales, q):
             queue.dma_start(plane[32 * q : 32 * q + 4, :].bitcast(I32), scales[0, 4 * q : 4 * q + 4, :].bitcast(I32))
 
         nc.sync.dma_start(offs_sb[:], offs)
-        nc.sync.dma_start(par_sb[:], par)
+        nc.sync.dma_start(xs_sb[112:P, :].bitcast(I32), x_scales[0].bitcast(I32))
         nc.sync.dma_start(s_raw[0][:], s_rows[:, :, 0:V_HALF])
-        nc.sync.dma_start(xs_sb[32:96:4, :].bitcast(I32), x_scales[0].bitcast(I32))
         nc.sync.dma_start(s_raw[1][:], s_rows[:, :, V_HALF:V])
         for q in range(4):
             load_scale_rows(nc.sync, w2s, w2_scales, q)
+        nc.sync.dma_start(par_sb[:], par)
         nc.sync.dma_start(xw_sb[:].bitcast(I32), x_words[0].rearrange("p n r -> p (n r)").bitcast(I32))
         for q in range(2, 4):
             load_scale_rows(nc.sync, w1s, w1_scales, q)
@@ -71,7 +71,7 @@ def tile_picked_fpn_relu_p_kernel(
             for q in range(4):
                 nc.sync.dma_start(
                     xs_plane[h][32 * q : 32 * q + 4, :].bitcast(I32),
-                    picked[32 + 16 * q : 48 + 16 * q : 4, :].bitcast(I32),
+                    picked[112 + 4 * q : 116 + 4 * q, :].bitcast(I32),
                 )
 
         pick_scales(0, "xs_picked0")
@@ -81,14 +81,12 @@ def tile_picked_fpn_relu_p_kernel(
         ]
         s_codes = [keep.tile([P, V_HALF], U32, name=f"s_codes{h}", align_bytes=64) for h in range(2)]
         s_scales = [keep.tile([P, V_HALF], U8, name=f"s_scales{h}", align_bytes=64) for h in range(2)]
-        for h, c0, c1, on_scalar in [(0, 0, 256, True), (1, 0, 128, True), (1, 128, 256, False)]:
-            dst = grouped[h][:, c0:c1, :].rearrange("p (c i) j -> p c j i", i=4)
-            src = s_raw[h][:, :, c0:c1].rearrange("p j (c i) -> p c j i", i=4)
-            if on_scalar:
-                nc.scalar.copy(dst, src)
-            else:
-                nc.vector.tensor_copy(dst, src)
-        for h in range(2):
+        for h, split in enumerate([128,96]):
+            for c0, c1, copy in [(0, split, nc.scalar.copy), (split, V_HALF, nc.vector.tensor_copy)]:
+                copy(
+                    grouped[h][:, c0:c1, :].rearrange("p (c i) j -> p c j i", i=4),
+                    s_raw[h][:, :, c0:c1].rearrange("p j (c i) -> p c j i", i=4),
+                )
             nc.vector.quantize_mx(
                 out=s_codes[h][:].bitcast(FP8X4),
                 scales=s_scales[h][:],

@@ -50,8 +50,8 @@ def tile_picked_fpn_relu_p_kernel(
         def load_scale_rows(queue, plane, scales, q):
             queue.dma_start(plane[32 * q : 32 * q + 4, :].bitcast(I32), scales[0, 4 * q : 4 * q + 4, :].bitcast(I32))
 
-        nc.sync.dma_start(offs_sb[:], offs)
         nc.sync.dma_start(xs_sb[112:P, :].bitcast(I32), x_scales[0].bitcast(I32))
+        nc.sync.dma_start(offs_sb[:], offs)
         nc.sync.dma_start(s_raw[0][:], s_rows[:, :, 0:V_HALF])
         nc.sync.dma_start(s_raw[1][:], s_rows[:, :, V_HALF:V])
         for q in range(4):
@@ -61,9 +61,9 @@ def tile_picked_fpn_relu_p_kernel(
         for q in range(2, 4):
             load_scale_rows(nc.sync, w1s, w1_scales, q)
         nc.gpsimd.dma_start(w2w[:].bitcast(I32), w2_words[0].bitcast(I32))
-        nc.gpsimd.dma_start(w1w[:].bitcast(I32), w1_words[0].bitcast(I32))
         for q in range(2):
             load_scale_rows(nc.gpsimd, w1s, w1_scales, q)
+        nc.gpsimd.dma_start(w1w[:].bitcast(I32), w1_words[0].bitcast(I32))
 
         def pick_scales(h, tag):
             picked = keep.tile([P, HALF], U8, name=f"xs_picked{h}", tag=tag, align_bytes=64)

@@ -21,7 +21,7 @@ PACK = 4
 GROUP = 16
 HALF = S // 2
 V_HALF = V // 2
-T_PAD = 16
+T_WINDOW = 1376
 
 
 def tile_picked_fpn_relu_p_kernel(
@@ -92,8 +92,8 @@ def tile_picked_fpn_relu_p_kernel(
                 scales=s_scales[h][:],
                 in_=grouped[h][:].rearrange("p c j -> p (c j)"),
             )
-        pick_scales(1, "grouped1")
-        t_sb = keep.tile([P, V + T_PAD], F32, name="t_sb", tag="s_raw1", align_bytes=64)
+        pick_scales(1, "grouped0")
+        t_sb = keep.tile([P, T_WINDOW], F32, name="t_sb", align_bytes=64)
         nc.vector.memset(t_sb[:, V:], 0.0)
         for h in range(2):
             t_ps = psum.tile([P, V_HALF], F32, name=f"t_ps{h}")
@@ -108,10 +108,9 @@ def tile_picked_fpn_relu_p_kernel(
             )
             nc.scalar.copy(t_sb[:, h * V_HALF : (h + 1) * V_HALF], t_ps[:])
 
-        t_picked = [keep.tile([P, HALF], F32, name=f"t_picked{h}", align_bytes=64) for h in range(2)]
+        t_picked = keep.tile([P, S], F32, name="t_picked", align_bytes=64)
         xw_picked = [keep.tile([P, HALF], U32, name=f"xw_picked{h}", align_bytes=64) for h in range(2)]
-        for h in range(2):
-            nc.vector.tensor_copy(t_picked[h][:], t_sb[:].indirect(par_sb[:, lists[h]]))
+        nc.vector.tensor_copy(t_picked[:], t_sb[:].indirect(par_sb[:]))
         for h in range(2):
             nc.vector.tensor_copy(xw_picked[h][:], xw_sb[:].indirect(offs_sb[:, lists[h]]))
 
@@ -129,7 +128,7 @@ def tile_picked_fpn_relu_p_kernel(
                 stop=True,
             )
             total = keep.tile([P, width], F32, name=f"total{i}", align_bytes=64)
-            nc.vector.tensor_tensor(total[:], y_ps[:], t_picked[h][:, c0 : c0 + width], ADD)
+            nc.vector.tensor_tensor(total[:], y_ps[:], t_picked[:, h * HALF + c0 : h * HALF + c0 + width], ADD)
             sums.append(total)
         for i, (h, c0, width) in enumerate(pieces):
             result = keep.tile([P, width], F32, name=f"result{i}", align_bytes=64)

@@ -50,7 +50,7 @@ def tile_picked_fpn_relu_p_kernel(
         def load_scale_rows(queue, plane, scales, q):
             queue.dma_start(plane[32 * q : 32 * q + 4, :].bitcast(I32), scales[0, 4 * q : 4 * q + 4, :].bitcast(I32))
 
-        nc.sync.dma_start(xs_sb[112:P, :].bitcast(I32), x_scales[0].bitcast(I32))
+        nc.scalar.dma_start(xs_sb[112:P, :].bitcast(I32), x_scales[0].bitcast(I32))
         nc.sync.dma_start(offs_sb[:], offs)
         nc.sync.dma_start(s_raw[0][:], s_rows[:, :, 0:V_HALF])
         nc.sync.dma_start(s_raw[1][:], s_rows[:, :, V_HALF:V])
@@ -58,12 +58,11 @@ def tile_picked_fpn_relu_p_kernel(
             load_scale_rows(nc.sync, w2s, w2_scales, q)
         nc.sync.dma_start(par_sb[:], par)
         nc.sync.dma_start(xw_sb[:].bitcast(I32), x_words[0].rearrange("p n r -> p (n r)").bitcast(I32))
-        for q in range(2, 4):
-            load_scale_rows(nc.sync, w1s, w1_scales, q)
+        nc.sync.dma_start(w1w[:].bitcast(I32), w1_words[0].bitcast(I32))
+        load_scale_rows(nc.sync, w1s, w1_scales, 3)
         nc.gpsimd.dma_start(w2w[:].bitcast(I32), w2_words[0].bitcast(I32))
-        for q in range(2):
+        for q in range(3):
             load_scale_rows(nc.gpsimd, w1s, w1_scales, q)
-        nc.gpsimd.dma_start(w1w[:].bitcast(I32), w1_words[0].bitcast(I32))
 
         def pick_scales(h, tag):
             picked = keep.tile([P, HALF], U8, name=f"xs_picked{h}", tag=tag, align_bytes=64)

@@ -21,7 +21,8 @@ PACK = 4
 GROUP = 16
 HALF = S // 2
 V_HALF = V // 2
-T_WINDOW = 1376
+T_WINDOW = 1024
+FUSED = 256
 
 
 def tile_picked_fpn_relu_p_kernel(
@@ -36,7 +37,7 @@ def tile_picked_fpn_relu_p_kernel(
         par_sb = keep.tile([P, S // GROUP], U16, name="par_sb")
         xw_sb = keep.tile([P, T], U32, name="xw_sb", align_bytes=64)
         xs_sb = keep.tile([P, T], U8, name="xs_sb", align_bytes=64)
-        s_raw = [keep.tile([P, PACK, V_HALF], F32, name=f"s_raw{h}", tag=f"s_raw{h}", align_bytes=64) for h in range(2)]
+        s_raw = keep.tile([P, PACK, V], F32, name="s_raw", align_bytes=64)
         w1w = keep.tile([P, 2 * N], U8, name="w1w", align_bytes=64)
         w2w = keep.tile([P, 2 * N], U8, name="w2w", align_bytes=64)
         w1s = keep.tile([P, N], U8, name="w1s", align_bytes=64)
@@ -52,8 +53,7 @@ def tile_picked_fpn_relu_p_kernel(
 
         nc.scalar.dma_start(xs_sb[112:P, :].bitcast(I32), x_scales[0].bitcast(I32))
         nc.sync.dma_start(offs_sb[:], offs)
-        nc.sync.dma_start(s_raw[0][:], s_rows[:, :, 0:V_HALF])
-        nc.sync.dma_start(s_raw[1][:], s_rows[:, :, V_HALF:V])
+        nc.sync.dma_start(s_raw[:], s_rows)
         for q in range(4):
             load_scale_rows(nc.sync, w2s, w2_scales, q)
         nc.sync.dma_start(par_sb[:], par)
@@ -80,18 +80,18 @@ def tile_picked_fpn_relu_p_kernel(
         ]
         s_codes = [keep.tile([P, V_HALF], U32, name=f"s_codes{h}", align_bytes=64) for h in range(2)]
         s_scales = [keep.tile([P, V_HALF], U8, name=f"s_scales{h}", align_bytes=64) for h in range(2)]
-        for h, split in enumerate([128,96]):
+        for h, split in enumerate([96, 128]):
             for c0, c1, copy in [(0, split, nc.scalar.copy), (split, V_HALF, nc.vector.tensor_copy)]:
                 copy(
                     grouped[h][:, c0:c1, :].rearrange("p (c i) j -> p c j i", i=4),
-                    s_raw[h][:, :, c0:c1].rearrange("p j (c i) -> p c j i", i=4),
+                    s_raw[:, :, h * V_HALF + c0 : h * V_HALF + c1].rearrange("p j (c i) -> p c j i", i=4),
                 )
             nc.vector.quantize_mx(
                 out=s_codes[h][:].bitcast(FP8X4),
                 scales=s_scales[h][:],
                 in_=grouped[h][:].rearrange("p c j -> p (c j)"),
             )
-        pick_scales(1, "grouped0")
+        pick_scales(1, "grouped1")
         t_sb = keep.tile([P, T_WINDOW], F32, name="t_sb", align_bytes=64)
         nc.vector.memset(t_sb[:, V:], 0.0)
         for h in range(2):
@@ -107,9 +107,9 @@ def tile_picked_fpn_relu_p_kernel(
             )
             nc.scalar.copy(t_sb[:, h * V_HALF : (h + 1) * V_HALF], t_ps[:])
 
-        t_picked = keep.tile([P, S], F32, name="t_picked", align_bytes=64)
+        t_picked = keep.tile([P, S - FUSED], F32, name="t_picked", align_bytes=64)
         xw_picked = [keep.tile([P, HALF], U32, name=f"xw_picked{h}", align_bytes=64) for h in range(2)]
-        nc.vector.tensor_copy(t_picked[:], t_sb[:].indirect(par_sb[:]))
+        nc.vector.tensor_copy(t_picked[:], t_sb[:].indirect(par_sb[:, FUSED // GROUP :]))
         for h in range(2):
             nc.vector.tensor_copy(xw_picked[h][:], xw_sb[:].indirect(offs_sb[:, lists[h]]))
 
@@ -127,7 +127,13 @@ def tile_picked_fpn_relu_p_kernel(
                 stop=True,
             )
             total = keep.tile([P, width], F32, name=f"total{i}", align_bytes=64)
-            nc.vector.tensor_tensor(total[:], y_ps[:], t_picked[:, h * HALF + c0 : h * HALF + c0 + width], ADD)
+            if i == 0:
+                y_sb = keep.tile([P, FUSED], F32, name="y_sb", align_bytes=64)
+                nc.scalar.copy(y_sb[:], y_ps[:])
+                nc.vector.tensor_tensor(total[:], t_sb[:].indirect(par_sb[:, : FUSED // GROUP]), y_sb[:], ADD)
+            else:
+                j0 = h * HALF + c0 - FUSED
+                nc.vector.tensor_tensor(total[:], y_ps[:], t_picked[:, j0 : j0 + width], ADD)
             sums.append(total)
         for i, (h, c0, width) in enumerate(pieces):
             result = keep.tile([P, width], F32, name=f"result{i}", align_bytes=64)

@@ -20,7 +20,8 @@ P = 128
 PACK = 4
 GROUP = 16
 HALF = S // 2
-V_HALF = V // 2
+V_PIECE = V // 4
+SCALAR_LAST = 72
 T_WINDOW = 1024
 FUSED = 256
 
@@ -76,36 +77,42 @@ def tile_picked_fpn_relu_p_kernel(
         pick_scales(0, "xs_picked0")
 
         grouped = [
-            keep.tile([P, V_HALF, PACK], BF16, name=f"grouped{h}", tag=f"grouped{h}", align_bytes=64) for h in range(2)
+            keep.tile([P, V_PIECE, PACK], BF16, name=f"grouped{i}", tag=f"grouped{i}", align_bytes=64) for i in range(4)
         ]
-        s_codes = [keep.tile([P, V_HALF], U32, name=f"s_codes{h}", align_bytes=64) for h in range(2)]
-        s_scales = [keep.tile([P, V_HALF], U8, name=f"s_scales{h}", align_bytes=64) for h in range(2)]
-        for h, split in enumerate([96, 128]):
-            for c0, c1, copy in [(0, split, nc.scalar.copy), (split, V_HALF, nc.vector.tensor_copy)]:
-                copy(
-                    grouped[h][:, c0:c1, :].rearrange("p (c i) j -> p c j i", i=4),
-                    s_raw[:, :, h * V_HALF + c0 : h * V_HALF + c1].rearrange("p j (c i) -> p c j i", i=4),
-                )
-            nc.vector.quantize_mx(
-                out=s_codes[h][:].bitcast(FP8X4),
-                scales=s_scales[h][:],
-                in_=grouped[h][:].rearrange("p c j -> p (c j)"),
+        s_codes = [keep.tile([P, V_PIECE], U32, name=f"s_codes{i}", align_bytes=64) for i in range(4)]
+        s_scales = [keep.tile([P, V_PIECE], U8, name=f"s_scales{i}", align_bytes=64) for i in range(4)]
+        for i, c0, c1, copy in [
+            (0, 0, V_PIECE, nc.vector.tensor_copy),
+            (1, 0, V_PIECE, nc.scalar.copy),
+            (2, 0, V_PIECE, nc.vector.tensor_copy),
+            (3, 0, SCALAR_LAST, nc.scalar.copy),
+            (3, SCALAR_LAST, V_PIECE, nc.vector.tensor_copy),
+        ]:
+            copy(
+                grouped[i][:, c0:c1, :].rearrange("p (c i) j -> p c j i", i=4),
+                s_raw[:, :, i * V_PIECE + c0 : i * V_PIECE + c1].rearrange("p j (c i) -> p c j i", i=4),
             )
-        pick_scales(1, "grouped1")
+        for i in (0, 1, 3, 2):
+            nc.vector.quantize_mx(
+                out=s_codes[i][:].bitcast(FP8X4),
+                scales=s_scales[i][:],
+                in_=grouped[i][:].rearrange("p c j -> p (c j)"),
+            )
+        pick_scales(1, "grouped3")
         t_sb = keep.tile([P, T_WINDOW], F32, name="t_sb", align_bytes=64)
         nc.vector.memset(t_sb[:, V:], 0.0)
-        for h in range(2):
-            t_ps = psum.tile([P, V_HALF], F32, name=f"t_ps{h}")
+        for i in (0, 1, 3, 2):
+            t_ps = psum.tile([P, V_PIECE], F32, name=f"t_ps{i}")
             nc.tensor.matmul_mx(
                 out=t_ps[:],
                 lhsT=w2w[:].bitcast(FP4X4),
                 lhsT_scale=w2s[:],
-                rhs=s_codes[h][:].bitcast(FP8X4),
-                rhs_scale=s_scales[h][:],
+                rhs=s_codes[i][:].bitcast(FP8X4),
+                rhs_scale=s_scales[i][:],
                 start=True,
                 stop=True,
             )
-            nc.scalar.copy(t_sb[:, h * V_HALF : (h + 1) * V_HALF], t_ps[:])
+            nc.scalar.copy(t_sb[:, i * V_PIECE : (i + 1) * V_PIECE], t_ps[:])
 
         t_picked = keep.tile([P, S - FUSED], F32, name="t_picked", align_bytes=64)
         xw_picked = [keep.tile([P, HALF], U32, name=f"xw_picked{h}", align_bytes=64) for h in range(2)]

@@ -23,7 +23,7 @@ HALF = S // 2
 V_PIECE = V // 4
 SCALAR_LAST = 72
 T_WINDOW = 1024
-FUSED = 256
+FUSED = 128
 
 
 def tile_picked_fpn_relu_p_kernel(
@@ -102,7 +102,7 @@ def tile_picked_fpn_relu_p_kernel(
         t_sb = keep.tile([P, T_WINDOW], F32, name="t_sb", align_bytes=64)
         nc.vector.memset(t_sb[:, V:], 0.0)
         for i in (0, 1, 3, 2):
-            t_ps = psum.tile([P, V_PIECE], F32, name=f"t_ps{i}")
+            t_ps = psum.tile([P, V_PIECE], F32, name=f"t_ps{i}", tag=f"bank{i + 4}")
             nc.tensor.matmul_mx(
                 out=t_ps[:],
                 lhsT=w2w[:].bitcast(FP4X4),
@@ -120,10 +120,13 @@ def tile_picked_fpn_relu_p_kernel(
         for h in range(2):
             nc.vector.tensor_copy(xw_picked[h][:], xw_sb[:].indirect(offs_sb[:, lists[h]]))
 
-        pieces = [(0, 0, 256), (0, 256, 256), (1, 0, 256), (1, 256, 256)]
-        sums = []
-        for i, (h, c0, width) in enumerate(pieces):
-            y_ps = psum.tile([P, width], F32, name=f"y_ps{i}")
+        pieces = [(0, 128), (128, 128), (256, 256), (512, 128), (640, 128), (768, 128), (896, 128)]
+        total = keep.tile([P, S], F32, name="total", align_bytes=64)
+        result = keep.tile([P, S], F32, name="result", align_bytes=64)
+        for i, (j0, width) in enumerate(pieces):
+            h, c0 = divmod(j0, HALF)
+            cols = slice(j0, j0 + width)
+            y_ps = psum.tile([P, width], F32, name=f"y_ps{i}", tag=f"bank{i}")
             nc.tensor.matmul_mx(
                 out=y_ps[:],
                 lhsT=w1w[:].bitcast(FP4X4),
@@ -133,19 +136,17 @@ def tile_picked_fpn_relu_p_kernel(
                 start=True,
                 stop=True,
             )
-            total = keep.tile([P, width], F32, name=f"total{i}", align_bytes=64)
             if i == 0:
                 y_sb = keep.tile([P, FUSED], F32, name="y_sb", align_bytes=64)
                 nc.scalar.copy(y_sb[:], y_ps[:])
-                nc.vector.tensor_tensor(total[:], t_sb[:].indirect(par_sb[:, : FUSED // GROUP]), y_sb[:], ADD)
+                nc.vector.tensor_tensor(total[:, cols], t_sb[:].indirect(par_sb[:, : FUSED // GROUP]), y_sb[:], ADD)
             else:
-                j0 = h * HALF + c0 - FUSED
-                nc.vector.tensor_tensor(total[:], y_ps[:], t_picked[:, j0 : j0 + width], ADD)
-            sums.append(total)
-        for i, (h, c0, width) in enumerate(pieces):
-            result = keep.tile([P, width], F32, name=f"result{i}", align_bytes=64)
-            if i < 3:
-                nc.scalar.activation(result[:], sums[i][:], RELU)
+                nc.vector.tensor_tensor(total[:, cols], y_ps[:], t_picked[:, j0 - FUSED : j0 - FUSED + width], ADD)
+        for j0, width, on_scalar in [(256, 256, True), (128, 128, True), (0, 128, True), (512, 128, True), (640, 128, True), (768, 128, False), (896, 128, False)]:
+            cols = slice(j0, j0 + width)
+            if on_scalar:
+                nc.scalar.activation(result[:, cols], total[:, cols], RELU)
             else:
-                nc.vector.tensor_scalar_max(result[:], sums[i][:], 0.0)
-            nc.sync.dma_start(out[:, h * HALF + c0 : h * HALF + c0 + width], result[:])
+                nc.vector.tensor_scalar_max(result[:, cols], total[:, cols], 0.0)
+        for j0, width in [(256, 256), (0, 256), (512, 256), (768, 256)]:
+            nc.sync.dma_start(out[:, j0 : j0 + width], result[:, j0 : j0 + width])

@@ -19,11 +19,18 @@ RELU = mybir.ActivationFunctionType.Relu
 P = 128
 PACK = 4
 GROUP = 16
+QUADS = 4
+QUAD = P // QUADS
+ROWS = K // 32 // QUADS
+XS_FIRST = P - K // 32
 HALF = S // 2
+LINE = 4
+
 V_PIECE = V // 4
-SCALAR_LAST = 72
+SCALAR_SHARE = 72
 T_WINDOW = 1024
 FUSED = 128
+NARROW, WIDE = 128, 256
 
 
 def tile_picked_fpn_relu_p_kernel(
@@ -44,34 +51,36 @@ def tile_picked_fpn_relu_p_kernel(
         w1s = keep.tile([P, N], U8, name="w1s", align_bytes=64)
         w2s = keep.tile([P, N], U8, name="w2s", align_bytes=64)
         xs_plane = [keep.tile([P, HALF], U8, name=f"xs_plane{h}", align_bytes=64) for h in range(2)]
-        lists = [slice(h * HALF // GROUP, (h + 1) * HALF // GROUP) for h in range(2)]
+        offs_cols = [slice(h * HALF // GROUP, (h + 1) * HALF // GROUP) for h in range(2)]
 
-        nc.vector.memset(xs_sb[0:112, :].bitcast(I32), 0)
+        nc.vector.memset(xs_sb[0:XS_FIRST, :].bitcast(I32), 0)
 
-        s_rows = sT.rearrange("(p j) v -> p j v", j=PACK)
         def load_scale_rows(queue, plane, scales, q):
-            queue.dma_start(plane[32 * q : 32 * q + 4, :].bitcast(I32), scales[0, 4 * q : 4 * q + 4, :].bitcast(I32))
+            queue.dma_start(
+                plane[QUAD * q : QUAD * q + ROWS, :].bitcast(I32),
+                scales[0, ROWS * q : ROWS * (q + 1), :].bitcast(I32),
+            )
 
-        nc.scalar.dma_start(xs_sb[112:P, :].bitcast(I32), x_scales[0].bitcast(I32))
+        nc.scalar.dma_start(xs_sb[XS_FIRST:P, :].bitcast(I32), x_scales[0].bitcast(I32))
         nc.sync.dma_start(offs_sb[:], offs)
-        nc.sync.dma_start(s_raw[:], s_rows)
-        for q in range(4):
+        nc.sync.dma_start(s_raw[:], sT.rearrange("(p j) v -> p j v", j=PACK))
+        nc.sync.dma_start(w2w[:].bitcast(I32), w2_words[0].bitcast(I32))
+        for q in range(QUADS):
             load_scale_rows(nc.sync, w2s, w2_scales, q)
         nc.sync.dma_start(par_sb[:], par)
         nc.sync.dma_start(xw_sb[:].bitcast(I32), x_words[0].rearrange("p n r -> p (n r)").bitcast(I32))
         nc.sync.dma_start(w1w[:].bitcast(I32), w1_words[0].bitcast(I32))
-        load_scale_rows(nc.sync, w1s, w1_scales, 3)
-        nc.gpsimd.dma_start(w2w[:].bitcast(I32), w2_words[0].bitcast(I32))
-        for q in range(3):
+        load_scale_rows(nc.sync, w1s, w1_scales, QUADS - 1)
+        for q in range(QUADS - 1):
             load_scale_rows(nc.gpsimd, w1s, w1_scales, q)
 
         def pick_scales(h, tag):
             picked = keep.tile([P, HALF], U8, name=f"xs_picked{h}", tag=tag, align_bytes=64)
-            nc.vector.tensor_copy(picked[:], xs_sb[:].indirect(offs_sb[:, lists[h]]))
-            for q in range(4):
+            nc.vector.tensor_copy(picked[:], xs_sb[:].indirect(offs_sb[:, offs_cols[h]]))
+            for q in range(QUADS):
                 nc.sync.dma_start(
-                    xs_plane[h][32 * q : 32 * q + 4, :].bitcast(I32),
-                    picked[112 + 4 * q : 116 + 4 * q, :].bitcast(I32),
+                    xs_plane[h][QUAD * q : QUAD * q + ROWS, :].bitcast(I32),
+                    picked[XS_FIRST + ROWS * q : XS_FIRST + ROWS * (q + 1), :].bitcast(I32),
                 )
 
         pick_scales(0, "xs_picked0")
@@ -85,23 +94,25 @@ def tile_picked_fpn_relu_p_kernel(
             (0, 0, V_PIECE, nc.vector.tensor_copy),
             (1, 0, V_PIECE, nc.scalar.copy),
             (2, 0, V_PIECE, nc.vector.tensor_copy),
-            (3, 0, SCALAR_LAST, nc.scalar.copy),
-            (3, SCALAR_LAST, V_PIECE, nc.vector.tensor_copy),
+            (3, 0, SCALAR_SHARE, nc.scalar.copy),
+            (3, SCALAR_SHARE, V_PIECE, nc.vector.tensor_copy),
         ]:
             copy(
-                grouped[i][:, c0:c1, :].rearrange("p (c i) j -> p c j i", i=4),
-                s_raw[:, :, i * V_PIECE + c0 : i * V_PIECE + c1].rearrange("p j (c i) -> p c j i", i=4),
+                grouped[i][:, c0:c1, :].rearrange("p (c i) j -> p c j i", i=LINE),
+                s_raw[:, :, i * V_PIECE + c0 : i * V_PIECE + c1].rearrange("p j (c i) -> p c j i", i=LINE),
             )
-        for i in (0, 1, 3, 2):
+        piece_order = (0, 1, 3, 2)
+        for i in piece_order:
             nc.vector.quantize_mx(
                 out=s_codes[i][:].bitcast(FP8X4),
                 scales=s_scales[i][:],
                 in_=grouped[i][:].rearrange("p c j -> p (c j)"),
             )
         pick_scales(1, "grouped3")
+
         t_sb = keep.tile([P, T_WINDOW], F32, name="t_sb", align_bytes=64)
         nc.vector.memset(t_sb[:, V:], 0.0)
-        for i in (0, 1, 3, 2):
+        for i in piece_order:
             t_ps = psum.tile([P, V_PIECE], F32, name=f"t_ps{i}", tag=f"bank{i + 4}")
             nc.tensor.matmul_mx(
                 out=t_ps[:],
@@ -118,12 +129,13 @@ def tile_picked_fpn_relu_p_kernel(
         xw_picked = [keep.tile([P, HALF], U32, name=f"xw_picked{h}", align_bytes=64) for h in range(2)]
         nc.vector.tensor_copy(t_picked[:], t_sb[:].indirect(par_sb[:, FUSED // GROUP :]))
         for h in range(2):
-            nc.vector.tensor_copy(xw_picked[h][:], xw_sb[:].indirect(offs_sb[:, lists[h]]))
+            nc.vector.tensor_copy(xw_picked[h][:], xw_sb[:].indirect(offs_sb[:, offs_cols[h]]))
 
-        pieces = [(0, 128), (128, 128), (256, 256), (512, 128), (640, 128), (768, 128), (896, 128)]
+        fused_piece, beside_piece, wide_piece = (0, FUSED), (FUSED, WIDE - FUSED), (WIDE, WIDE)
+        late_pieces = [(j0, NARROW) for j0 in range(HALF, S, NARROW)]
         total = keep.tile([P, S], F32, name="total", align_bytes=64)
         result = keep.tile([P, S], F32, name="result", align_bytes=64)
-        for i, (j0, width) in enumerate(pieces):
+        for i, (j0, width) in enumerate([fused_piece, beside_piece, wide_piece] + late_pieces):
             h, c0 = divmod(j0, HALF)
             cols = slice(j0, j0 + width)
             y_ps = psum.tile([P, width], F32, name=f"y_ps{i}", tag=f"bank{i}")
@@ -136,17 +148,17 @@ def tile_picked_fpn_relu_p_kernel(
                 start=True,
                 stop=True,
             )
-            if i == 0:
+            if j0 < FUSED:
                 y_sb = keep.tile([P, FUSED], F32, name="y_sb", align_bytes=64)
                 nc.scalar.copy(y_sb[:], y_ps[:])
                 nc.vector.tensor_tensor(total[:, cols], t_sb[:].indirect(par_sb[:, : FUSED // GROUP]), y_sb[:], ADD)
             else:
                 nc.vector.tensor_tensor(total[:, cols], y_ps[:], t_picked[:, j0 - FUSED : j0 - FUSED + width], ADD)
-        for j0, width, on_scalar in [(256, 256, True), (128, 128, True), (0, 128, True), (512, 128, True), (640, 128, True), (768, 128, False), (896, 128, False)]:
-            cols = slice(j0, j0 + width)
-            if on_scalar:
-                nc.scalar.activation(result[:, cols], total[:, cols], RELU)
-            else:
-                nc.vector.tensor_scalar_max(result[:, cols], total[:, cols], 0.0)
-        for j0, width in [(256, 256), (0, 256), (512, 256), (768, 256)]:
-            nc.sync.dma_start(out[:, j0 : j0 + width], result[:, j0 : j0 + width])
+
+        for j0, width in [wide_piece, beside_piece, fused_piece] + late_pieces[:2]:
+            nc.scalar.activation(result[:, j0 : j0 + width], total[:, j0 : j0 + width], RELU)
+        for j0, width in late_pieces[2:]:
+            nc.vector.tensor_scalar_max(result[:, j0 : j0 + width], total[:, j0 : j0 + width], 0.0)
+
+        for j0 in (WIDE, 0, HALF, HALF + WIDE):
+            nc.sync.dma_start(out[:, j0 : j0 + WIDE], result[:, j0 : j0 + WIDE])

@@ -14,6 +14,7 @@ U8 = mybir.dt.uint8
 FP8X4 = mybir.dt.float8_e4m3fn_x4
 FP4X4 = mybir.dt.float4_e2m1fn_x4
 ADD = mybir.AluOpType.add
+COPY = mybir.ActivationFunctionType.Copy
 RELU = mybir.ActivationFunctionType.Relu
 
 P = 128
@@ -28,8 +29,7 @@ LINE = 4
 
 V_PIECE = V // 4
 SCALAR_SHARE = 72
-T_WINDOW = 1024
-FUSED = 128
+PAR_VECTOR = 384
 NARROW, WIDE = 128, 256
 
 
@@ -50,7 +50,7 @@ def tile_picked_fpn_relu_p_kernel(
         w2w = keep.tile([P, 2 * N], U8, name="w2w", align_bytes=64)
         w1s = keep.tile([P, N], U8, name="w1s", align_bytes=64)
         w2s = keep.tile([P, N], U8, name="w2s", align_bytes=64)
-        xs_plane = [keep.tile([P, HALF], U8, name=f"xs_plane{h}", align_bytes=64) for h in range(2)]
+        xs_plane = keep.tile([P, S], U8, name="xs_plane", align_bytes=64)
         offs_cols = [slice(h * HALF // GROUP, (h + 1) * HALF // GROUP) for h in range(2)]
 
         nc.vector.memset(xs_sb[0:XS_FIRST, :].bitcast(I32), 0)
@@ -70,20 +70,18 @@ def tile_picked_fpn_relu_p_kernel(
         nc.sync.dma_start(par_sb[:], par)
         nc.sync.dma_start(xw_sb[:].bitcast(I32), x_words[0].rearrange("p n r -> p (n r)").bitcast(I32))
         nc.sync.dma_start(w1w[:].bitcast(I32), w1_words[0].bitcast(I32))
-        load_scale_rows(nc.sync, w1s, w1_scales, QUADS - 1)
-        for q in range(QUADS - 1):
+        for q in range(QUADS // 2, QUADS):
+            load_scale_rows(nc.sync, w1s, w1_scales, q)
+        for q in range(QUADS // 2):
             load_scale_rows(nc.gpsimd, w1s, w1_scales, q)
 
-        def pick_scales(h, tag):
-            picked = keep.tile([P, HALF], U8, name=f"xs_picked{h}", tag=tag, align_bytes=64)
-            nc.vector.tensor_copy(picked[:], xs_sb[:].indirect(offs_sb[:, offs_cols[h]]))
-            for q in range(QUADS):
-                nc.sync.dma_start(
-                    xs_plane[h][QUAD * q : QUAD * q + ROWS, :].bitcast(I32),
-                    picked[XS_FIRST + ROWS * q : XS_FIRST + ROWS * (q + 1), :].bitcast(I32),
-                )
-
-        pick_scales(0, "xs_picked0")
+        xs_picked = keep.tile([P, S], U8, name="xs_picked", align_bytes=64)
+        nc.vector.tensor_copy(xs_picked[:], xs_sb[:].indirect(offs_sb[:]))
+        for q in range(QUADS):
+            nc.sync.dma_start(
+                xs_plane[QUAD * q : QUAD * q + ROWS, :].bitcast(I32),
+                xs_picked[XS_FIRST + ROWS * q : XS_FIRST + ROWS * (q + 1), :].bitcast(I32),
+            )
 
         grouped = [
             keep.tile([P, V_PIECE, PACK], BF16, name=f"grouped{i}", tag=f"grouped{i}", align_bytes=64) for i in range(4)
@@ -108,10 +106,8 @@ def tile_picked_fpn_relu_p_kernel(
                 scales=s_scales[i][:],
                 in_=grouped[i][:].rearrange("p c j -> p (c j)"),
             )
-        pick_scales(1, "grouped3")
 
-        t_sb = keep.tile([P, T_WINDOW], F32, name="t_sb", align_bytes=64)
-        nc.vector.memset(t_sb[:, V:], 0.0)
+        t_sb = keep.tile([P, V], F32, name="t_sb", align_bytes=64)
         for i in piece_order:
             t_ps = psum.tile([P, V_PIECE], F32, name=f"t_ps{i}", tag=f"bank{i + 4}")
             nc.tensor.matmul_mx(
@@ -125,17 +121,21 @@ def tile_picked_fpn_relu_p_kernel(
             )
             nc.scalar.copy(t_sb[:, i * V_PIECE : (i + 1) * V_PIECE], t_ps[:])
 
-        t_picked = keep.tile([P, S - FUSED], F32, name="t_picked", align_bytes=64)
+        t_picked = keep.tile([P, S], F32, name="t_picked", align_bytes=64)
         xw_picked = [keep.tile([P, HALF], U32, name=f"xw_picked{h}", align_bytes=64) for h in range(2)]
-        nc.vector.tensor_copy(t_picked[:], t_sb[:].indirect(par_sb[:, FUSED // GROUP :]))
+        par_scalar = (S - PAR_VECTOR) // 2
+        for j0 in (0, par_scalar):
+            nc.scalar.activation(
+                t_picked[:, j0 : j0 + par_scalar], t_sb[:].indirect(par_sb[:, j0 // GROUP : (j0 + par_scalar) // GROUP]), COPY
+            )
+        nc.vector.tensor_copy(t_picked[:, S - PAR_VECTOR :], t_sb[:].indirect(par_sb[:, (S - PAR_VECTOR) // GROUP :]))
         for h in range(2):
             nc.vector.tensor_copy(xw_picked[h][:], xw_sb[:].indirect(offs_sb[:, offs_cols[h]]))
 
-        fused_piece, beside_piece, wide_piece = (0, FUSED), (FUSED, WIDE - FUSED), (WIDE, WIDE)
-        late_pieces = [(j0, NARROW) for j0 in range(HALF, S, NARROW)]
+        pieces = [(0, WIDE), (WIDE, WIDE)] + [(j0, NARROW) for j0 in range(HALF, S, NARROW)]
         total = keep.tile([P, S], F32, name="total", align_bytes=64)
         result = keep.tile([P, S], F32, name="result", align_bytes=64)
-        for i, (j0, width) in enumerate([fused_piece, beside_piece, wide_piece] + late_pieces):
+        for i, (j0, width) in enumerate(pieces):
             h, c0 = divmod(j0, HALF)
             cols = slice(j0, j0 + width)
             y_ps = psum.tile([P, width], F32, name=f"y_ps{i}", tag=f"bank{i}")
@@ -144,21 +144,16 @@ def tile_picked_fpn_relu_p_kernel(
                 lhsT=w1w[:].bitcast(FP4X4),
                 lhsT_scale=w1s[:],
                 rhs=xw_picked[h][:, c0 : c0 + width].bitcast(FP8X4),
-                rhs_scale=xs_plane[h][:, c0 : c0 + width],
+                rhs_scale=xs_plane[:, cols],
                 start=True,
                 stop=True,
             )
-            if j0 < FUSED:
-                y_sb = keep.tile([P, FUSED], F32, name="y_sb", align_bytes=64)
-                nc.scalar.copy(y_sb[:], y_ps[:])
-                nc.vector.tensor_tensor(total[:, cols], t_sb[:].indirect(par_sb[:, : FUSED // GROUP]), y_sb[:], ADD)
-            else:
-                nc.vector.tensor_tensor(total[:, cols], y_ps[:], t_picked[:, j0 - FUSED : j0 - FUSED + width], ADD)
+            nc.vector.tensor_tensor(total[:, cols], y_ps[:], t_picked[:, cols], ADD)
 
-        for j0, width in [wide_piece, beside_piece, fused_piece] + late_pieces[:2]:
+        for j0, width in pieces[:4]:
             nc.scalar.activation(result[:, j0 : j0 + width], total[:, j0 : j0 + width], RELU)
-        for j0, width in late_pieces[2:]:
+        for j0, width in pieces[4:]:
             nc.vector.tensor_scalar_max(result[:, j0 : j0 + width], total[:, j0 : j0 + width], 0.0)
 
-        for j0 in (WIDE, 0, HALF, HALF + WIDE):
+        for j0 in range(0, S, WIDE):
             nc.sync.dma_start(out[:, j0 : j0 + WIDE], result[:, j0 : j0 + WIDE])

@@ -24,13 +24,13 @@ QUADS = 4
 QUAD = P // QUADS
 ROWS = K // 32 // QUADS
 XS_FIRST = P - K // 32
-HALF = S // 2
 LINE = 4
 
 V_PIECE = V // 4
 SCALAR_SHARE = 72
 PAR_VECTOR = 384
-NARROW, WIDE = 128, 256
+PAR_SCALAR = (S - PAR_VECTOR) // 2
+HALF, QUARTER, EIGHTH = S // 2, S // 4, S // 8
 
 
 def tile_picked_fpn_relu_p_kernel(
@@ -51,9 +51,11 @@ def tile_picked_fpn_relu_p_kernel(
         w1s = keep.tile([P, N], U8, name="w1s", align_bytes=64)
         w2s = keep.tile([P, N], U8, name="w2s", align_bytes=64)
         xs_plane = keep.tile([P, S], U8, name="xs_plane", align_bytes=64)
-        offs_cols = [slice(h * HALF // GROUP, (h + 1) * HALF // GROUP) for h in range(2)]
 
         nc.vector.memset(xs_sb[0:XS_FIRST, :].bitcast(I32), 0)
+
+        def list_columns(j0, width):
+            return slice(j0 // GROUP, (j0 + width) // GROUP)
 
         def load_scale_rows(queue, plane, scales, q):
             queue.dma_start(
@@ -84,10 +86,10 @@ def tile_picked_fpn_relu_p_kernel(
             )
 
         grouped = [
-            keep.tile([P, V_PIECE, PACK], BF16, name=f"grouped{i}", tag=f"grouped{i}", align_bytes=64) for i in range(4)
+            keep.tile([P, V_PIECE, PACK], BF16, name=f"grouped{i}", align_bytes=64) for i in range(V // V_PIECE)
         ]
-        s_codes = [keep.tile([P, V_PIECE], U32, name=f"s_codes{i}", align_bytes=64) for i in range(4)]
-        s_scales = [keep.tile([P, V_PIECE], U8, name=f"s_scales{i}", align_bytes=64) for i in range(4)]
+        s_codes = [keep.tile([P, V_PIECE], U32, name=f"s_codes{i}", align_bytes=64) for i in range(V // V_PIECE)]
+        s_scales = [keep.tile([P, V_PIECE], U8, name=f"s_scales{i}", align_bytes=64) for i in range(V // V_PIECE)]
         for i, c0, c1, copy in [
             (0, 0, V_PIECE, nc.vector.tensor_copy),
             (1, 0, V_PIECE, nc.scalar.copy),
@@ -122,38 +124,67 @@ def tile_picked_fpn_relu_p_kernel(
             nc.scalar.copy(t_sb[:, i * V_PIECE : (i + 1) * V_PIECE], t_ps[:])
 
         t_picked = keep.tile([P, S], F32, name="t_picked", align_bytes=64)
-        xw_picked = [keep.tile([P, HALF], U32, name=f"xw_picked{h}", align_bytes=64) for h in range(2)]
-        par_scalar = (S - PAR_VECTOR) // 2
-        for j0 in (0, par_scalar):
+        for j0 in (0, PAR_SCALAR):
             nc.scalar.activation(
-                t_picked[:, j0 : j0 + par_scalar], t_sb[:].indirect(par_sb[:, j0 // GROUP : (j0 + par_scalar) // GROUP]), COPY
+                t_picked[:, j0 : j0 + PAR_SCALAR], t_sb[:].indirect(par_sb[:, list_columns(j0, PAR_SCALAR)]), COPY
             )
-        nc.vector.tensor_copy(t_picked[:, S - PAR_VECTOR :], t_sb[:].indirect(par_sb[:, (S - PAR_VECTOR) // GROUP :]))
-        for h in range(2):
-            nc.vector.tensor_copy(xw_picked[h][:], xw_sb[:].indirect(offs_sb[:, offs_cols[h]]))
+        nc.vector.tensor_copy(
+            t_picked[:, S - PAR_VECTOR :], t_sb[:].indirect(par_sb[:, list_columns(S - PAR_VECTOR, PAR_VECTOR)])
+        )
 
-        pieces = [(0, WIDE), (WIDE, WIDE)] + [(j0, NARROW) for j0 in range(HALF, S, NARROW)]
+        gathers = [(0, HALF), (HALF, QUARTER), (HALF + QUARTER, QUARTER)]
+        xw_picked = [keep.tile([P, width], U32, name=f"xw_picked{j0}", align_bytes=64) for j0, width in gathers]
+        for g, (j0, width) in enumerate(gathers):
+            nc.vector.tensor_copy(xw_picked[g][:], xw_sb[:].indirect(offs_sb[:, list_columns(j0, width)]))
+
         total = keep.tile([P, S], F32, name="total", align_bytes=64)
         result = keep.tile([P, S], F32, name="result", align_bytes=64)
-        for i, (j0, width) in enumerate(pieces):
-            h, c0 = divmod(j0, HALF)
-            cols = slice(j0, j0 + width)
-            y_ps = psum.tile([P, width], F32, name=f"y_ps{i}", tag=f"bank{i}")
+
+        def columns(piece):
+            return slice(piece[0], piece[0] + piece[1])
+
+        def product(bank, g, piece):
+            j0, width = piece
+            c0 = j0 - gathers[g][0]
+            y_ps = psum.tile([P, width], F32, name=f"y_ps{bank}", tag=f"bank{bank}")
             nc.tensor.matmul_mx(
                 out=y_ps[:],
                 lhsT=w1w[:].bitcast(FP4X4),
                 lhsT_scale=w1s[:],
-                rhs=xw_picked[h][:, c0 : c0 + width].bitcast(FP8X4),
-                rhs_scale=xs_plane[:, cols],
+                rhs=xw_picked[g][:, c0 : c0 + width].bitcast(FP8X4),
+                rhs_scale=xs_plane[:, columns(piece)],
                 start=True,
                 stop=True,
             )
-            nc.vector.tensor_tensor(total[:, cols], y_ps[:], t_picked[:, cols], ADD)
+            return y_ps
 
-        for j0, width in pieces[:4]:
-            nc.scalar.activation(result[:, j0 : j0 + width], total[:, j0 : j0 + width], RELU)
-        for j0, width in pieces[4:]:
-            nc.vector.tensor_scalar_max(result[:, j0 : j0 + width], total[:, j0 : j0 + width], 0.0)
+        def add_on_vector(bank, g, piece):
+            y_ps = product(bank, g, piece)
+            nc.vector.tensor_tensor(total[:, columns(piece)], y_ps[:], t_picked[:, columns(piece)], ADD)
 
-        for j0 in range(0, S, WIDE):
-            nc.sync.dma_start(out[:, j0 : j0 + WIDE], result[:, j0 : j0 + WIDE])
+        def relu_on_vector(piece):
+            nc.vector.tensor_scalar_max(result[:, columns(piece)], total[:, columns(piece)], 0.0)
+
+        first, second = (0, EIGHTH), (EIGHTH, EIGHTH)
+        third, fourth = (QUARTER, QUARTER), (HALF, QUARTER)
+        fifth, sixth = (S - QUARTER, EIGHTH), (S - EIGHTH, EIGHTH)
+
+        y_first = product(0, 0, first)
+        y_sb = keep.tile([P, EIGHTH], F32, name="y_sb", align_bytes=64)
+        nc.scalar.copy(y_sb[:], y_first[:])
+        nc.gpsimd.tensor_tensor(total[:, columns(first)], y_sb[:], t_picked[:, columns(first)], ADD)
+
+        add_on_vector(1, 0, second)
+        add_on_vector(2, 0, third)
+        add_on_vector(3, 1, fourth)
+        add_on_vector(4, 2, fifth)
+        relu_on_vector(fourth)
+        add_on_vector(5, 2, sixth)
+
+        for piece in (second, first, third):
+            nc.scalar.activation(result[:, columns(piece)], total[:, columns(piece)], RELU)
+        for piece in (fifth, sixth):
+            relu_on_vector(piece)
+
+        for piece in (second, first, third, fourth, fifth, sixth):
+            nc.sync.dma_start(out[:, columns(piece)], result[:, columns(piece)])

@@ -132,19 +132,19 @@ def tile_picked_fpn_relu_p_kernel(
             t_picked[:, S - PAR_VECTOR :], t_sb[:].indirect(par_sb[:, list_columns(S - PAR_VECTOR, PAR_VECTOR)])
         )
 
-        gathers = [(0, HALF), (HALF, QUARTER), (HALF + QUARTER, QUARTER)]
+        gathers = [(j0, QUARTER) for j0 in range(0, S, QUARTER)]
         xw_picked = [keep.tile([P, width], U32, name=f"xw_picked{j0}", align_bytes=64) for j0, width in gathers]
         for g, (j0, width) in enumerate(gathers):
             nc.vector.tensor_copy(xw_picked[g][:], xw_sb[:].indirect(offs_sb[:, list_columns(j0, width)]))
 
-        total = keep.tile([P, S], F32, name="total", align_bytes=64)
         result = keep.tile([P, S], F32, name="result", align_bytes=64)
 
         def columns(piece):
             return slice(piece[0], piece[0] + piece[1])
 
-        def product(bank, g, piece):
+        def product(bank, piece):
             j0, width = piece
+            g = max(i for i, (first, unused) in enumerate(gathers) if first <= j0)
             c0 = j0 - gathers[g][0]
             y_ps = psum.tile([P, width], F32, name=f"y_ps{bank}", tag=f"bank{bank}")
             nc.tensor.matmul_mx(
@@ -158,33 +158,34 @@ def tile_picked_fpn_relu_p_kernel(
             )
             return y_ps
 
-        def add_on_vector(bank, g, piece):
-            y_ps = product(bank, g, piece)
-            nc.vector.tensor_tensor(total[:, columns(piece)], y_ps[:], t_picked[:, columns(piece)], ADD)
+        pieces = [(0, EIGHTH), (EIGHTH, EIGHTH), (QUARTER, QUARTER), (HALF, QUARTER)]
+        pieces = pieces + [(S - QUARTER, EIGHTH), (S - EIGHTH, EIGHTH)]
+        y_ps = [product(bank, piece) for bank, piece in enumerate(pieces)]
+        early = keep.tile([P, QUARTER], F32, name="early", align_bytes=64)
+        sums = {}
+        for k in range(2):
+            y_sb = keep.tile([P, EIGHTH], F32, name=f"y_sb{k}", tag=f"y_sb{k}", align_bytes=64)
+            nc.scalar.copy(y_sb[:], y_ps[k][:])
+            sums[k] = early[:, columns(pieces[k])]
+            nc.gpsimd.tensor_tensor(sums[k], y_sb[:], t_picked[:, columns(pieces[k])], ADD)
+        late = keep.tile([P, S - QUARTER], F32, name="late", tag="y_sb0", align_bytes=64)
+        for k in (2, 3, 4, 5):
+            sums[k] = late[:, pieces[k][0] - QUARTER : pieces[k][0] - QUARTER + pieces[k][1]]
 
-        def relu_on_vector(piece):
-            nc.vector.tensor_scalar_max(result[:, columns(piece)], total[:, columns(piece)], 0.0)
+        def add_on_vector(k):
+            nc.vector.tensor_tensor(sums[k], y_ps[k][:], t_picked[:, columns(pieces[k])], ADD)
 
-        first, second = (0, EIGHTH), (EIGHTH, EIGHTH)
-        third, fourth = (QUARTER, QUARTER), (HALF, QUARTER)
-        fifth, sixth = (S - QUARTER, EIGHTH), (S - EIGHTH, EIGHTH)
+        def relu_on_vector(k):
+            nc.vector.tensor_scalar_max(result[:, columns(pieces[k])], sums[k], 0.0)
 
-        y_first = product(0, 0, first)
-        y_sb = keep.tile([P, EIGHTH], F32, name="y_sb", align_bytes=64)
-        nc.scalar.copy(y_sb[:], y_first[:])
-        nc.gpsimd.tensor_tensor(total[:, columns(first)], y_sb[:], t_picked[:, columns(first)], ADD)
-
-        add_on_vector(1, 0, second)
-        add_on_vector(2, 0, third)
-        add_on_vector(3, 1, fourth)
-        add_on_vector(4, 2, fifth)
-        relu_on_vector(fourth)
-        add_on_vector(5, 2, sixth)
-
-        for piece in (second, first, third):
-            nc.scalar.activation(result[:, columns(piece)], total[:, columns(piece)], RELU)
-        for piece in (fifth, sixth):
-            relu_on_vector(piece)
-
-        for piece in (second, first, third, fourth, fifth, sixth):
+        add_on_vector(2)
+        add_on_vector(3)
+        relu_on_vector(1)
+        for k in (4, 5):
+            add_on_vector(k)
+        for k in (4, 5):
+            relu_on_vector(k)
+        for k in (0, 2, 3):
+            nc.scalar.activation(result[:, columns(pieces[k])], sums[k], RELU)
+        for piece in pieces[:4] + [(S - QUARTER, QUARTER)]:
             nc.sync.dma_start(out[:, columns(piece)], result[:, columns(piece)])

@@ -187,5 +187,5 @@ def tile_picked_fpn_relu_p_kernel(
             relu_on_vector(k)
         for k in (0, 2, 3):
             nc.scalar.activation(result[:, columns(pieces[k])], sums[k], RELU)
-        for piece in pieces[:4] + [(S - QUARTER, QUARTER)]:
+        for piece in pieces:
             nc.sync.dma_start(out[:, columns(piece)], result[:, columns(piece)])

@@ -65,17 +65,17 @@ def tile_picked_fpn_relu_p_kernel(
 
         nc.scalar.dma_start(xs_sb[XS_FIRST:P, :].bitcast(I32), x_scales[0].bitcast(I32))
         nc.sync.dma_start(offs_sb[:], offs)
-        nc.sync.dma_start(s_raw[:], sT.rearrange("(p j) v -> p j v", j=PACK))
+        nc.sync.dma_start(par_sb[:], par)
         nc.sync.dma_start(w2w[:].bitcast(I32), w2_words[0].bitcast(I32))
+        nc.sync.dma_start(s_raw[:], sT.rearrange("(p j) v -> p j v", j=PACK))
         for q in range(QUADS):
             load_scale_rows(nc.sync, w2s, w2_scales, q)
-        nc.sync.dma_start(par_sb[:], par)
+        for q in range(QUADS // 2):
+            load_scale_rows(nc.sync, w1s, w1_scales, q)
         nc.sync.dma_start(xw_sb[:].bitcast(I32), x_words[0].rearrange("p n r -> p (n r)").bitcast(I32))
         nc.sync.dma_start(w1w[:].bitcast(I32), w1_words[0].bitcast(I32))
         for q in range(QUADS // 2, QUADS):
             load_scale_rows(nc.sync, w1s, w1_scales, q)
-        for q in range(QUADS // 2):
-            load_scale_rows(nc.gpsimd, w1s, w1_scales, q)
 
         xs_picked = keep.tile([P, S], U8, name="xs_picked", align_bytes=64)
         nc.vector.tensor_copy(xs_picked[:], xs_sb[:].indirect(offs_sb[:]))
@@ -187,5 +187,5 @@ def tile_picked_fpn_relu_p_kernel(
             relu_on_vector(k)
         for k in (0, 2, 3):
             nc.scalar.activation(result[:, columns(pieces[k])], sums[k], RELU)
-        for piece in pieces:
+        for piece in pieces[:4] + [(S - QUARTER, QUARTER)]:
             nc.sync.dma_start(out[:, columns(piece)], result[:, columns(piece)])

@@ -69,7 +69,7 @@ def tile_picked_fpn_relu_p_kernel(
         nc.sync.dma_start(w2w[:].bitcast(I32), w2_words[0].bitcast(I32))
         nc.sync.dma_start(s_raw[:], sT.rearrange("(p j) v -> p j v", j=PACK))
         for q in range(QUADS):
-            load_scale_rows(nc.sync, w2s, w2_scales, q)
+            load_scale_rows(nc.scalar, w2s, w2_scales, q)
         for q in range(QUADS // 2):
             load_scale_rows(nc.sync, w1s, w1_scales, q)
         nc.sync.dma_start(xw_sb[:].bitcast(I32), x_words[0].rearrange("p n r -> p (n r)").bitcast(I32))

@@ -66,10 +66,10 @@ def tile_picked_fpn_relu_p_kernel(
         nc.scalar.dma_start(xs_sb[XS_FIRST:P, :].bitcast(I32), x_scales[0].bitcast(I32))
         nc.sync.dma_start(offs_sb[:], offs)
         nc.sync.dma_start(par_sb[:], par)
-        nc.sync.dma_start(w2w[:].bitcast(I32), w2_words[0].bitcast(I32))
-        nc.sync.dma_start(s_raw[:], sT.rearrange("(p j) v -> p j v", j=PACK))
+        nc.scalar.dma_start(w2w[:].bitcast(I32), w2_words[0].bitcast(I32))
+        nc.scalar.dma_start(s_raw[:], sT.rearrange("(p j) v -> p j v", j=PACK))
         for q in range(QUADS):
-            load_scale_rows(nc.scalar, w2s, w2_scales, q)
+            load_scale_rows(nc.sync, w2s, w2_scales, q)
         for q in range(QUADS // 2):
             load_scale_rows(nc.sync, w1s, w1_scales, q)
         nc.sync.dma_start(xw_sb[:].bitcast(I32), x_words[0].rearrange("p n r -> p (n r)").bitcast(I32))

from contextlib import ExitStack

import concourse.mybir as mybir

K, T, S, V, N = 512, 4096, 1024, 512, 128
FLOPS = 2 * K * N * (S + V)

F32 = mybir.dt.float32
BF16 = mybir.dt.bfloat16
I32 = mybir.dt.int32
U32 = mybir.dt.uint32
U16 = mybir.dt.uint16
U8 = mybir.dt.uint8
FP8X4 = mybir.dt.float8_e4m3fn_x4
FP4X4 = mybir.dt.float4_e2m1fn_x4
ADD = mybir.AluOpType.add
COPY = mybir.ActivationFunctionType.Copy
RELU = mybir.ActivationFunctionType.Relu

P = 128
PACK = 4
GROUP = 16
QUADS = 4
QUAD = P // QUADS
ROWS = K // 32 // QUADS
XS_FIRST = P - K // 32
LINE = 4

V_PIECE = V // 4
SCALAR_SHARE = 72
PAR_VECTOR = 384
PAR_SCALAR = (S - PAR_VECTOR) // 2
HALF, QUARTER, EIGHTH = S // 2, S // 4, S // 8


def tile_picked_fpn_relu_p_kernel(
    tc, x_words, x_scales, sT, w1_words, w1_scales, w2_words, w2_scales, offs, par, out
):
    nc = tc.nc
    with ExitStack() as ctx:
        keep = ctx.enter_context(tc.tile_pool(name="keep", bufs=1))
        psum = ctx.enter_context(tc.psum_pool(name="psum", bufs=1))

        offs_sb = keep.tile([P, S // GROUP], U16, name="offs_sb")
        par_sb = keep.tile([P, S // GROUP], U16, name="par_sb")
        xw_sb = keep.tile([P, T], U32, name="xw_sb", align_bytes=64)
        xs_sb = keep.tile([P, T], U8, name="xs_sb", align_bytes=64)
        s_raw = keep.tile([P, PACK, V], F32, name="s_raw", align_bytes=64)
        w1w = keep.tile([P, 2 * N], U8, name="w1w", align_bytes=64)
        w2w = keep.tile([P, 2 * N], U8, name="w2w", align_bytes=64)
        w1s = keep.tile([P, N], U8, name="w1s", align_bytes=64)
        w2s = keep.tile([P, N], U8, name="w2s", align_bytes=64)
        xs_plane = keep.tile([P, S], U8, name="xs_plane", align_bytes=64)

        nc.vector.memset(xs_sb[0:XS_FIRST, :].bitcast(I32), 0)

        def list_columns(j0, width):
            return slice(j0 // GROUP, (j0 + width) // GROUP)

        def load_scale_rows(queue, plane, scales, q):
            queue.dma_start(
                plane[QUAD * q : QUAD * q + ROWS, :].bitcast(I32),
                scales[0, ROWS * q : ROWS * (q + 1), :].bitcast(I32),
            )

        nc.scalar.dma_start(xs_sb[XS_FIRST:P, :].bitcast(I32), x_scales[0].bitcast(I32))
        nc.sync.dma_start(offs_sb[:], offs)
        nc.sync.dma_start(par_sb[:], par)
        nc.scalar.dma_start(w2w[:].bitcast(I32), w2_words[0].bitcast(I32))
        nc.scalar.dma_start(s_raw[:], sT.rearrange("(p j) v -> p j v", j=PACK))
        for q in range(QUADS):
            load_scale_rows(nc.sync, w2s, w2_scales, q)
        for q in range(QUADS // 2):
            load_scale_rows(nc.sync, w1s, w1_scales, q)
        nc.sync.dma_start(xw_sb[:].bitcast(I32), x_words[0].rearrange("p n r -> p (n r)").bitcast(I32))
        nc.sync.dma_start(w1w[:].bitcast(I32), w1_words[0].bitcast(I32))
        for q in range(QUADS // 2, QUADS):
            load_scale_rows(nc.sync, w1s, w1_scales, q)

        xs_picked = keep.tile([P, S], U8, name="xs_picked", align_bytes=64)
        nc.vector.tensor_copy(xs_picked[:], xs_sb[:].indirect(offs_sb[:]))
        for q in range(QUADS):
            nc.sync.dma_start(
                xs_plane[QUAD * q : QUAD * q + ROWS, :].bitcast(I32),
                xs_picked[XS_FIRST + ROWS * q : XS_FIRST + ROWS * (q + 1), :].bitcast(I32),
            )

        grouped = [
            keep.tile([P, V_PIECE, PACK], BF16, name=f"grouped{i}", align_bytes=64) for i in range(V // V_PIECE)
        ]
        s_codes = [keep.tile([P, V_PIECE], U32, name=f"s_codes{i}", align_bytes=64) for i in range(V // V_PIECE)]
        s_scales = [keep.tile([P, V_PIECE], U8, name=f"s_scales{i}", align_bytes=64) for i in range(V // V_PIECE)]
        for i, c0, c1, copy in [
            (0, 0, V_PIECE, nc.vector.tensor_copy),
            (1, 0, V_PIECE, nc.scalar.copy),
            (2, 0, V_PIECE, nc.vector.tensor_copy),
            (3, 0, SCALAR_SHARE, nc.scalar.copy),
            (3, SCALAR_SHARE, V_PIECE, nc.vector.tensor_copy),
        ]:
            copy(
                grouped[i][:, c0:c1, :].rearrange("p (c i) j -> p c j i", i=LINE),
                s_raw[:, :, i * V_PIECE + c0 : i * V_PIECE + c1].rearrange("p j (c i) -> p c j i", i=LINE),
            )
        piece_order = (0, 1, 3, 2)
        for i in piece_order:
            nc.vector.quantize_mx(
                out=s_codes[i][:].bitcast(FP8X4),
                scales=s_scales[i][:],
                in_=grouped[i][:].rearrange("p c j -> p (c j)"),
            )

        t_sb = keep.tile([P, V], F32, name="t_sb", align_bytes=64)
        for i in piece_order:
            t_ps = psum.tile([P, V_PIECE], F32, name=f"t_ps{i}", tag=f"bank{i + 4}")
            nc.tensor.matmul_mx(
                out=t_ps[:],
                lhsT=w2w[:].bitcast(FP4X4),
                lhsT_scale=w2s[:],
                rhs=s_codes[i][:].bitcast(FP8X4),
                rhs_scale=s_scales[i][:],
                start=True,
                stop=True,
            )
            nc.scalar.copy(t_sb[:, i * V_PIECE : (i + 1) * V_PIECE], t_ps[:])

        t_picked = keep.tile([P, S], F32, name="t_picked", align_bytes=64)
        for j0 in (0, PAR_SCALAR):
            nc.scalar.activation(
                t_picked[:, j0 : j0 + PAR_SCALAR], t_sb[:].indirect(par_sb[:, list_columns(j0, PAR_SCALAR)]), COPY
            )
        nc.vector.tensor_copy(
            t_picked[:, S - PAR_VECTOR :], t_sb[:].indirect(par_sb[:, list_columns(S - PAR_VECTOR, PAR_VECTOR)])
        )

        gathers = [(j0, QUARTER) for j0 in range(0, S, QUARTER)]
        xw_picked = [keep.tile([P, width], U32, name=f"xw_picked{j0}", align_bytes=64) for j0, width in gathers]
        for g, (j0, width) in enumerate(gathers):
            nc.vector.tensor_copy(xw_picked[g][:], xw_sb[:].indirect(offs_sb[:, list_columns(j0, width)]))

        result = keep.tile([P, S], F32, name="result", align_bytes=64)

        def columns(piece):
            return slice(piece[0], piece[0] + piece[1])

        def product(bank, piece):
            j0, width = piece
            g = max(i for i, (first, unused) in enumerate(gathers) if first <= j0)
            c0 = j0 - gathers[g][0]
            y_ps = psum.tile([P, width], F32, name=f"y_ps{bank}", tag=f"bank{bank}")
            nc.tensor.matmul_mx(
                out=y_ps[:],
                lhsT=w1w[:].bitcast(FP4X4),
                lhsT_scale=w1s[:],
                rhs=xw_picked[g][:, c0 : c0 + width].bitcast(FP8X4),
                rhs_scale=xs_plane[:, columns(piece)],
                start=True,
                stop=True,
            )
            return y_ps

        pieces = [(0, EIGHTH), (EIGHTH, EIGHTH), (QUARTER, QUARTER), (HALF, QUARTER)]
        pieces = pieces + [(S - QUARTER, EIGHTH), (S - EIGHTH, EIGHTH)]
        y_ps = [product(bank, piece) for bank, piece in enumerate(pieces)]
        early = keep.tile([P, QUARTER], F32, name="early", align_bytes=64)
        sums = {}
        for k in range(2):
            y_sb = keep.tile([P, EIGHTH], F32, name=f"y_sb{k}", tag=f"y_sb{k}", align_bytes=64)
            nc.scalar.copy(y_sb[:], y_ps[k][:])
            sums[k] = early[:, columns(pieces[k])]
            nc.gpsimd.tensor_tensor(sums[k], y_sb[:], t_picked[:, columns(pieces[k])], ADD)
        late = keep.tile([P, S - QUARTER], F32, name="late", tag="y_sb0", align_bytes=64)
        for k in (2, 3, 4, 5):
            sums[k] = late[:, pieces[k][0] - QUARTER : pieces[k][0] - QUARTER + pieces[k][1]]

        def add_on_vector(k):
            nc.vector.tensor_tensor(sums[k], y_ps[k][:], t_picked[:, columns(pieces[k])], ADD)

        def relu_on_vector(k):
            nc.vector.tensor_scalar_max(result[:, columns(pieces[k])], sums[k], 0.0)

        add_on_vector(2)
        add_on_vector(3)
        relu_on_vector(1)
        for k in (4, 5):
            add_on_vector(k)
        for k in (4, 5):
            relu_on_vector(k)
        for k in (0, 2, 3):
            nc.scalar.activation(result[:, columns(pieces[k])], sums[k], RELU)
        for piece in pieces[:4] + [(S - QUARTER, QUARTER)]:
            nc.sync.dma_start(out[:, columns(piece)], result[:, columns(piece)])
